import numpy as np
import ml_dtypes


def mxq(x, axis, fmt="e4m3"):
    dtype, down = {"e4m3": (ml_dtypes.float8_e4m3fn, 7), "e5m2": (ml_dtypes.float8_e5m2, 14)}[fmt]
    v = np.moveaxis(np.asarray(x, np.float32).astype(ml_dtypes.bfloat16).astype(np.float64), axis, -1)
    blocks = v.reshape(v.shape[:-1] + (-1, 32))
    amax = np.abs(blocks).max(-1, keepdims=True)
    byte = np.maximum(np.where(amax > 0, np.frexp(amax)[1] - 1 + 127, 0) - down, 1)
    scale = np.exp2(byte - 127.0)
    codes = (blocks / scale).astype(np.float32).astype(dtype).astype(np.float64)
    return np.moveaxis((codes * scale).reshape(v.shape), -1, axis)


WIDE = False


def mx_kscale(k):
    if not WIDE:
        return np.ones(k)
    levels = np.array([24, -24, 12, -12, 0])
    if k % 512:
        return np.exp2(np.random.permutation(np.resize(levels, k // 32))).repeat(32)
    a = np.empty((k // 512, 16))
    for p in range(k // 512):
        a[p, :8] = np.random.permutation(np.resize(levels, 8))
        for g in range(8):
            far = levels[np.abs(levels - a[p, g]) >= 10]
            a[p, g + 8] = far[np.random.randint(len(far))]
    return np.exp2(a.ravel()).repeat(32)


def f64(x):
    return np.asarray(x).astype(np.float64)


def striped(idx):
    return np.tile(idx.reshape(-1, 16).T, (8, 1)).astype(np.uint16)


def unstriped(offs):
    return offs[:16].T.reshape(-1).astype(np.int64)


E2M1 = np.array([0.0, 0.5, 1.0, 1.5, 2.0, 3.0, 4.0, 6.0, -0.0, -0.5, -1.0, -1.5, -2.0, -3.0, -4.0, -6.0])


def pack_weight(w, fmt):
    k, n = w.shape
    w = f64(np.asarray(w, np.float32).astype(ml_dtypes.bfloat16)).reshape(k // 32, 32, n)
    amax = np.abs(w).max(1)
    if fmt == "e4m3":
        byte = np.frexp(amax)[1] - 1 + 127 - 7
    else:
        mant, ex = np.frexp(amax / 6.0)
        byte = np.where(mant > 0.5, ex, ex - 1) + 127
    byte = np.clip(np.where(amax > 0, byte, 1), 1, 254)
    scaled = (w * np.exp2(127.0 - byte)[:, None, :]).reshape(k, n).astype(np.float32)
    by_word = np.ascontiguousarray(scaled.reshape(k // 512, 128, 4, n).transpose(0, 1, 3, 2))
    if fmt == "e4m3":
        words = by_word.astype(ml_dtypes.float8_e4m3fn).view(np.uint8)
    else:
        c = by_word.astype(ml_dtypes.float4_e2m1fn).view(np.uint8) & 0xF
        words = (c[..., 0::2] | (c[..., 1::2] << 4)).reshape(k // 512, 128, 2 * n)
    return np.ascontiguousarray(words), np.ascontiguousarray(byte.astype(np.uint8).reshape(k // 512, 16, n))


def unpack_weight(words, scales, fmt):
    g, _, n = scales.shape
    words = np.ascontiguousarray(words).reshape(g, 128, n, -1)
    if fmt == "e4m3":
        vals = words.view(ml_dtypes.float8_e4m3fn).astype(np.float64)
    else:
        nib = np.empty((g, 128, n, 4), np.uint8)
        nib[..., 0::2] = words & 0xF
        nib[..., 1::2] = words >> 4
        vals = E2M1[nib]
    vals = vals * np.repeat(np.exp2(scales.astype(np.float64) - 127.0), 8, axis=1)[..., None]
    return vals.transpose(0, 1, 3, 2).reshape(g * 512, n)


K, R, N, T, J = 512, 512, 512, 4096, 512


def setup_inputs():
    n = np.random.standard_normal
    s = mx_kscale(K)[:, None]
    u = mx_kscale(R)[:, None]
    p_tab = pack_weight(n((K, T)) * s, "e4m3")
    p_w = pack_weight(n((K, R)) / np.sqrt(K) / s * u.T, "e2m1")
    return {
        "tab_words": p_tab[0],
        "tab_scales": p_tab[1],
        "c": (n((K, J)) * s).astype(np.float32),
        "w_words": p_w[0],
        "w_scales": p_w[1],
        "wc": (n((K, R)) / np.sqrt(K) / s * u.T).astype(np.float32),
        "wd": (n((R, N)) / np.sqrt(R) / u).astype(np.float32),
        "b": (0.3 * n(N)).astype(np.float32),
        "offs": striped(np.concatenate([np.random.permutation(T)[:J] for _ in range(4)])),
    }


def reference(tab_words, tab_scales, c, w_words, w_scales, wc, wd, b, offs):
    idx = unstriped(offs).reshape(4, J)
    tab_ = unpack_weight(tab_words, tab_scales, "e4m3")[:, idx]
    c_ = mxq(f64(c), 0, "e4m3")
    w_ = unpack_weight(w_words, w_scales, "e2m1")
    a0 = w_.T @ tab_[:, 0]
    a1 = w_.T @ tab_[:, 1]
    a2 = w_.T @ tab_[:, 2]
    a3 = w_.T @ tab_[:, 3]
    wc_ = mxq(f64(wc), 0, "e4m3")
    ac = wc_.T @ c_
    h = np.maximum(np.maximum(np.maximum(np.maximum(a0, a1), a2), a3) + ac, 0.0)
    h_ = mxq(h, 0, "e4m3")
    wd_ = mxq(f64(wd), 0, "e4m3")
    y = wd_.T @ h_
    return y + f64(b)[:, None]

@@ -1,0 +1,255 @@
+from contextlib import ExitStack
+
+import concourse.mybir as mybir
+from concourse.masks import make_identity
+
+K, R, N, T, J, G = 512, 512, 512, 4096, 512, 4
+FLOPS = 2 * K * R * J * (G + 1) + 2 * R * N * J
+
+F32 = mybir.dt.float32
+BF16 = mybir.dt.bfloat16
+I32 = mybir.dt.int32
+U32 = mybir.dt.uint32
+U16 = mybir.dt.uint16
+U8 = mybir.dt.uint8
+FP8X4 = mybir.dt.float8_e4m3fn_x4
+FP4X4 = mybir.dt.float4_e2m1fn_x4
+ALU = mybir.AluOpType
+ACT = mybir.ActivationFunctionType
+
+P = 128
+PACK = 4
+CH = 128
+CHUNKS = J // CH
+HALF = 256
+
+
+def tile_list_pnet_bias_kernel(
+    tc, tab_words, tab_scales, c, w_words, w_scales, wc, wd, b, offs, out
+):
+    nc = tc.nc
+    with ExitStack() as ctx:
+        sb = ctx.enter_context(tc.tile_pool(name="sb", bufs=1))
+        ps = ctx.enter_context(tc.psum_pool(name="ps", bufs=1))
+
+        def tile(name, shape, dtype):
+            return sb.tile(shape, dtype, name=name, align_bytes=64)
+
+        offsets = sb.tile([P, G * J // 16], U16, name="offsets")
+        tab_plane = tile("tab_plane", [P, T // 4], I32)
+        tab_codes = tile("tab_codes", [P, T], I32)
+        w_plane = tile("w_plane", [P, R // 4], I32)
+        w_codes = tile("w_codes", [P, R // 2], I32)
+        bias = tile("bias", [P, N // P], F32)
+        ident = tile("ident", [P, P], F32)
+
+        nc.vector.memset(tab_plane[0 : P - 16, :], 0)
+
+        nc.sync.dma_start(offsets[:], offs)
+        nc.sync.dma_start(tab_plane[P - 16 : P, :], tab_scales[0].bitcast(I32))
+        for q in range(4):
+            nc.gpsimd.dma_start(w_plane[32 * q : 32 * q + 4, :], w_scales[0, 4 * q : 4 * q + 4, :].bitcast(I32))
+
+        def load_rows(name, src):
+            raw = tile(name, [P, PACK, src.shape[1]], F32)
+            nc.sync.dma_start(raw[:], src.rearrange("(p i) x -> p i x", i=PACK))
+            return raw
+
+        wc_raw = [load_rows("wc_raw0", wc[:, 0:HALF])]
+        nc.sync.dma_start(tab_codes[:], tab_words[0].rearrange("p t i -> p (t i)").bitcast(I32))
+        nc.sync.dma_start(w_codes[:], w_words[0].bitcast(I32))
+        wc_raw.append(load_rows("wc_raw1", wc[:, HALF:R]))
+        c_raw = [load_rows("c_raw%d" % u, c[:, HALF * u : HALF * (u + 1)]) for u in range(2)]
+        wd_raw = load_rows("wd_raw", wd)
+        with nc.allow_non_contiguous_dma(reason="one bias value a partition"):
+            nc.sync.dma_start(bias[:], b.rearrange("(q p) -> p q", p=P))
+
+        make_identity(nc, ident[:])
+
+        def woven(dst, src):
+            return (
+                dst.rearrange("p (x u) i -> p x i u", u=4),
+                src.rearrange("p i (x u) -> p x i u", u=4),
+            )
+
+        def quantize(codes, plane, src):
+            nc.vector.quantize_mx(out=codes.bitcast(FP8X4), scales=plane, in_=src.rearrange("p x i -> p (x i)"))
+
+        got_rows = tile("got_rows", [P, G * J], U8)
+        got_plane = tile("got_plane", [P, G * J], U8)
+        got_codes = [tile("got_codes%d" % g, [P, J], U32) for g in range(G)]
+
+        def gather_scales():
+            nc.vector.tensor_copy(got_rows[:], tab_plane[:].bitcast(U8).indirect(offsets[:]))
+            for q in range(4):
+                rows = slice(P - 16 + 4 * q, P - 16 + 4 * q + 4)
+                nc.scalar.dma_start(got_plane[32 * q : 32 * q + 4, :].bitcast(I32), got_rows[rows, :].bitcast(I32))
+
+        def gather_codes(g):
+            cols = slice(g * J // 16, (g + 1) * J // 16)
+            nc.vector.tensor_copy(got_codes[g][:], tab_codes[:].bitcast(U32).indirect(offsets[:, cols]))
+
+        s_banks = [ps.tile([P, R], F32, name="s_bank%d" % i) for i in range(2)]
+        v_banks = [ps.tile([P, R], F32, name="v_bank%d" % i) for i in range(3)]
+        h_banks = [ps.tile([P, PACK, CH], F32, name="h_bank%d" % i) for i in range(2)]
+        y_bank = ps.tile([P, R], F32, name="y_bank")
+
+        pooled = [
+            c_raw[k // 2][:, 2 * (k % 2) : 2 * (k % 2) + 2, :].rearrange("p a (e q) -> p (a e) q", q=P)
+            for k in range(CHUNKS)
+        ]
+        own = [tile("own%d" % k, [P, PACK, P], F32) for k in range(CHUNKS)]
+        wc_bf = [tile("wc_bf%d" % u, [P, HALF, PACK], BF16) for u in range(2)]
+        c_bf = [tile("c_bf%d" % u, [P, HALF, PACK], BF16) for u in range(2)]
+        wd_bf = tile("wd_bf", [P, N, PACK], BF16)
+        wc_codes = tile("wc_codes", [P, R], U32)
+        wc_plane = tile("wc_plane", [P, R], U8)
+        c_codes = [tile("c_codes%d" % u, [P, HALF], U32) for u in range(2)]
+        c_plane = [tile("c_plane%d" % u, [P, HALF], U8) for u in range(2)]
+        wd_codes = tile("wd_codes", [P, N], U32)
+        wd_plane = tile("wd_plane", [P, N], U8)
+        h_bf = [tile("h_bf%d" % k, [P, CH, PACK], BF16) for k in range(CHUNKS)]
+        h_codes = [tile("h_codes%d" % k, [P, CH], U32) for k in range(CHUNKS)]
+        h_plane = [tile("h_plane%d" % k, [P, CH], U8) for k in range(CHUNKS)]
+
+        def dealt(bank):
+            return bank[:].rearrange("p (q t) -> p t q", t=PACK)
+
+        def project(bank, g, k):
+            nc.tensor.matmul_mx(
+                out=bank[:],
+                lhsT=got_codes[g][:, CH * k : CH * (k + 1)].bitcast(FP8X4),
+                lhsT_scale=got_plane[:, J * g + CH * k : J * g + CH * (k + 1)],
+                rhs=w_codes[:].bitcast(U8).bitcast(FP4X4),
+                rhs_scale=w_plane[:].bitcast(U8),
+                start=True,
+                stop=True,
+            )
+
+        def first_neighbour(k):
+            bank = s_banks[k % 2]
+            project(bank, 0, k)
+            nc.scalar.copy(pooled[k], dealt(bank))
+
+        turns = []
+
+        def pool_in(k, g):
+            bank = v_banks[len(turns) % 3]
+            turns.append((k, g))
+            project(bank, g, k)
+            nc.vector.tensor_tensor(pooled[k], dealt(bank), pooled[k], ALU.max)
+
+        def round_wc(u):
+            nc.scalar.copy(*woven(wc_bf[u][:], wc_raw[u][:]))
+
+        def quantize_wc(u):
+            cols = slice(HALF * u, HALF * (u + 1))
+            quantize(wc_codes[:, cols], wc_plane[:, cols], wc_bf[u][:])
+
+        def round_c(u):
+            nc.scalar.copy(*woven(c_bf[u][:], c_raw[u][:]))
+
+        def quantize_c(u):
+            quantize(c_codes[u][:], c_plane[u][:], c_bf[u][:])
+
+        def own_projection(k):
+            bank = s_banks[k % 2]
+            cols = slice(CH * (k % 2), CH * (k % 2 + 1))
+            nc.tensor.matmul_mx(
+                out=bank[:],
+                lhsT=c_codes[k // 2][:, cols].bitcast(FP8X4),
+                lhsT_scale=c_plane[k // 2][:, cols],
+                rhs=wc_codes[:].bitcast(FP8X4),
+                rhs_scale=wc_plane[:],
+                start=True,
+                stop=True,
+            )
+            nc.scalar.copy(own[k][:], dealt(bank))
+
+        def turn(k):
+            bank = h_banks[k % 2]
+            for s, src in enumerate((own[k], pooled[k])):
+                for t in range(PACK):
+                    nc.tensor.matmul(
+                        bank[:, t, :], src[:, t, :], ident[:], is_transpose=True,
+                        start=(s == 0 and t == 0), stop=(s == 1 and t == PACK - 1),
+                    )
+            nc.scalar.activation(h_bf[k][:], bank[:].rearrange("p t j -> p j t"), ACT.Relu)
+
+        out_rows = out.rearrange("(q p) j -> p q j", p=P)
+
+        def output_rows(k, bank, q):
+            cols = slice(P * q, P * (q + 1))
+            nc.tensor.matmul_mx(
+                out=bank[:, CH * q : CH * (q + 1)],
+                lhsT=wd_codes[:, cols].bitcast(FP8X4),
+                lhsT_scale=wd_plane[:, cols],
+                rhs=h_codes[k][:].bitcast(FP8X4),
+                rhs_scale=h_plane[k][:],
+                start=True,
+                stop=True,
+            )
+
+        def add_bias_scalar(dst, bank, q):
+            nc.scalar.activation(dst, bank[:, CH * q : CH * (q + 1)], ACT.Identity, bias=bias[:, q : q + 1])
+
+        def add_bias_vector(dst, bank, q):
+            nc.vector.tensor_scalar(dst, bank[:, CH * q : CH * (q + 1)], bias[:, q : q + 1], None, ALU.add)
+
+        def second_layer(k, shares):
+            quantize(h_codes[k][:], h_plane[k][:], h_bf[k][:])
+            for bank, add_bias, qs in shares:
+                for q in qs:
+                    output_rows(k, bank, q)
+            for bank, add_bias, qs in shares:
+                result = tile("result%d_%d" % (k, qs[0]), [P, len(qs), CH], F32)
+                for i, q in enumerate(qs):
+                    add_bias(result[:, i, :], bank, q)
+                nc.sync.dma_start(out_rows[:, qs[0] : qs[-1] + 1, CH * k : CH * (k + 1)], result[:])
+
+        round_wc(0)
+        gather_scales()
+        quantize_wc(0)
+        for g in range(G):
+            gather_codes(g)
+        round_wc(1)
+
+        for q in range(N // P):
+            cols = slice(P * q, P * (q + 1))
+            dst, src = woven(wd_bf[:, cols, :], wd_raw[:, :, cols])
+            nc.gpsimd.tensor_scalar(dst, src, 1.0, 0.0, ALU.mult, ALU.add)
+
+        round_c(0)
+        first_neighbour(0)
+        first_neighbour(1)
+        quantize_wc(1)
+        quantize_c(0)
+        round_c(1)
+        pool_in(0, 1)
+        pool_in(1, 1)
+        first_neighbour(2)
+        own_projection(0)
+        pool_in(0, 2)
+        pool_in(1, 2)
+        first_neighbour(3)
+        quantize_c(1)
+        pool_in(0, 3)
+        pool_in(2, 1)
+        own_projection(1)
+        turn(0)
+        pool_in(1, 3)
+        pool_in(2, 2)
+        own_projection(2)
+        turn(1)
+        quantize(wd_codes[:], wd_plane[:], wd_bf[:])
+        pool_in(3, 1)
+        second_layer(0, [(y_bank, add_bias_scalar, [0, 1, 2, 3])])
+        pool_in(2, 3)
+        own_projection(3)
+        pool_in(3, 2)
+        second_layer(1, [(s_banks[0], add_bias_scalar, [0, 1, 2, 3])])
+        turn(2)
+        pool_in(3, 3)
+        turn(3)
+        second_layer(2, [(y_bank, add_bias_scalar, [0, 1, 2, 3])])
+        second_layer(3, [(s_banks[1], add_bias_scalar, [0, 1]), (v_banks[0], add_bias_vector, [2, 3])])

@@ -22,6 +22,7 @@ PACK = 4
 CH = 128
 CHUNKS = J // CH
 HALF = 256
+V_BANKS = 4
 
 
 def tile_list_pnet_bias_kernel(
@@ -43,12 +44,11 @@ def tile_list_pnet_bias_kernel(
         bias = tile("bias", [P, N // P], F32)
         ident = tile("ident", [P, P], F32)
 
+        make_identity(nc, ident[:])
         nc.vector.memset(tab_plane[0 : P - 16, :], 0)
 
         nc.sync.dma_start(offsets[:], offs)
         nc.sync.dma_start(tab_plane[P - 16 : P, :], tab_scales[0].bitcast(I32))
-        for q in range(4):
-            nc.gpsimd.dma_start(w_plane[32 * q : 32 * q + 4, :], w_scales[0, 4 * q : 4 * q + 4, :].bitcast(I32))
 
         def load_rows(name, src):
             raw = tile(name, [P, PACK, src.shape[1]], F32)
@@ -57,14 +57,15 @@ def tile_list_pnet_bias_kernel(
 
         wc_raw = [load_rows("wc_raw0", wc[:, 0:HALF])]
         nc.sync.dma_start(tab_codes[:], tab_words[0].rearrange("p t i -> p (t i)").bitcast(I32))
+        for q in range(4):
+            nc.sync.dma_start(w_plane[32 * q : 32 * q + 4, :], w_scales[0, 4 * q : 4 * q + 4, :].bitcast(I32))
         nc.sync.dma_start(w_codes[:], w_words[0].bitcast(I32))
         wc_raw.append(load_rows("wc_raw1", wc[:, HALF:R]))
         c_raw = [load_rows("c_raw%d" % u, c[:, HALF * u : HALF * (u + 1)]) for u in range(2)]
         wd_raw = load_rows("wd_raw", wd)
         with nc.allow_non_contiguous_dma(reason="one bias value a partition"):
-            nc.sync.dma_start(bias[:], b.rearrange("(q p) -> p q", p=P))
+            nc.gpsimd.dma_start(bias[:], b.rearrange("(q p) -> p q", p=P))
 
-        make_identity(nc, ident[:])
 
         def woven(dst, src):
             return (
@@ -90,9 +91,8 @@ def tile_list_pnet_bias_kernel(
             nc.vector.tensor_copy(got_codes[g][:], tab_codes[:].bitcast(U32).indirect(offsets[:, cols]))
 
         s_banks = [ps.tile([P, R], F32, name="s_bank%d" % i) for i in range(2)]
-        v_banks = [ps.tile([P, R], F32, name="v_bank%d" % i) for i in range(3)]
-        h_banks = [ps.tile([P, PACK, CH], F32, name="h_bank%d" % i) for i in range(2)]
-        y_bank = ps.tile([P, R], F32, name="y_bank")
+        v_banks = [ps.tile([P, R], F32, name="v_bank%d" % i) for i in range(V_BANKS)]
+        h_banks = [ps.tile([P, R], F32, name="h_bank%d" % i) for i in range(2)]
 
         pooled = [
             c_raw[k // 2][:, 2 * (k % 2) : 2 * (k % 2) + 2, :].rearrange("p a (e q) -> p (a e) q", q=P)
@@ -134,7 +134,7 @@ def tile_list_pnet_bias_kernel(
         turns = []
 
         def pool_in(k, g):
-            bank = v_banks[len(turns) % 3]
+            bank = v_banks[len(turns) % V_BANKS]
             turns.append((k, g))
             project(bank, g, k)
             nc.vector.tensor_tensor(pooled[k], dealt(bank), pooled[k], ALU.max)
@@ -166,15 +166,17 @@ def tile_list_pnet_bias_kernel(
             )
             nc.scalar.copy(own[k][:], dealt(bank))
 
-        def turn(k):
-            bank = h_banks[k % 2]
-            for s, src in enumerate((own[k], pooled[k])):
-                for t in range(PACK):
-                    nc.tensor.matmul(
-                        bank[:, t, :], src[:, t, :], ident[:], is_transpose=True,
-                        start=(s == 0 and t == 0), stop=(s == 1 and t == PACK - 1),
-                    )
-            nc.scalar.activation(h_bf[k][:], bank[:].rearrange("p t j -> p j t"), ACT.Relu)
+        def turn(bank, src, opens):
+            for t in range(PACK):
+                nc.tensor.matmul(
+                    bank[:, CH * t : CH * (t + 1)], src[:, t, :], ident[:], is_transpose=True,
+                    start=(opens and t == 0), stop=(not opens and t == PACK - 1),
+                )
+
+        def hidden(k, bank):
+            turn(bank, own[k], True)
+            turn(bank, pooled[k], False)
+            nc.scalar.activation(h_bf[k][:], bank[:].rearrange("p (t j) -> p j t", t=PACK), ACT.Relu)
 
         out_rows = out.rearrange("(q p) j -> p q j", p=P)
 
@@ -190,22 +192,25 @@ def tile_list_pnet_bias_kernel(
                 stop=True,
             )
 
-        def add_bias_scalar(dst, bank, q):
-            nc.scalar.activation(dst, bank[:, CH * q : CH * (q + 1)], ACT.Identity, bias=bias[:, q : q + 1])
+        def add_bias_scalar(dst, bank, lo, hi):
+            for q in range(lo, hi):
+                nc.scalar.activation(dst[:, q - lo, :], bank[:, CH * q : CH * (q + 1)], ACT.Identity, bias=bias[:, q : q + 1])
 
-        def add_bias_vector(dst, bank, q):
-            nc.vector.tensor_scalar(dst, bank[:, CH * q : CH * (q + 1)], bias[:, q : q + 1], None, ALU.add)
+        def add_bias_vector(dst, bank, lo, hi):
+            sums = bank[:, CH * lo : CH * hi].rearrange("p (q j) -> p q j", j=CH)
+            nc.vector.tensor_tensor(dst[:], sums, bias[:, lo:hi].unsqueeze(2).to_broadcast([P, hi - lo, CH]), ALU.add)
+
+        def quantize_h(k):
+            quantize(h_codes[k][:], h_plane[k][:], h_bf[k][:])
 
         def second_layer(k, shares):
-            quantize(h_codes[k][:], h_plane[k][:], h_bf[k][:])
-            for bank, add_bias, qs in shares:
-                for q in qs:
+            for bank, add_bias, lo, hi in shares:
+                for q in range(lo, hi):
                     output_rows(k, bank, q)
-            for bank, add_bias, qs in shares:
-                result = tile("result%d_%d" % (k, qs[0]), [P, len(qs), CH], F32)
-                for i, q in enumerate(qs):
-                    add_bias(result[:, i, :], bank, q)
-                nc.sync.dma_start(out_rows[:, qs[0] : qs[-1] + 1, CH * k : CH * (k + 1)], result[:])
+            for bank, add_bias, lo, hi in shares:
+                result = tile("result%d_%d" % (k, lo), [P, hi - lo, CH], F32)
+                add_bias(result, bank, lo, hi)
+                nc.sync.dma_start(out_rows[:, lo:hi, CH * k : CH * (k + 1)], result[:])
 
         round_wc(0)
         gather_scales()
@@ -214,42 +219,47 @@ def tile_list_pnet_bias_kernel(
             gather_codes(g)
         round_wc(1)
 
-        for q in range(N // P):
-            cols = slice(P * q, P * (q + 1))
-            dst, src = woven(wd_bf[:, cols, :], wd_raw[:, :, cols])
-            nc.gpsimd.tensor_scalar(dst, src, 1.0, 0.0, ALU.mult, ALU.add)
+        def round_wd(copy, lo, hi):
+            copy(*woven(wd_bf[:, lo:hi, :], wd_raw[:, :, lo:hi]))
 
         round_c(0)
         first_neighbour(0)
         first_neighbour(1)
         quantize_wc(1)
         quantize_c(0)
+        own_projection(0)
         round_c(1)
+        own_projection(1)
         pool_in(0, 1)
         pool_in(1, 1)
         first_neighbour(2)
-        own_projection(0)
         pool_in(0, 2)
         pool_in(1, 2)
         first_neighbour(3)
-        quantize_c(1)
         pool_in(0, 3)
+        quantize_c(1)
         pool_in(2, 1)
-        own_projection(1)
-        turn(0)
+        round_wd(nc.scalar.copy, 0 * P, 1 * P)
+        round_wd(nc.scalar.copy, 1 * P, 2 * P)
+        round_wd(nc.vector.tensor_copy, 2 * P, 4 * P)
+        quantize(wd_codes[:], wd_plane[:], wd_bf[:])
+        own_projection(2)
+        hidden(0, h_banks[0])
         pool_in(1, 3)
         pool_in(2, 2)
-        own_projection(2)
-        turn(1)
-        quantize(wd_codes[:], wd_plane[:], wd_bf[:])
-        pool_in(3, 1)
-        second_layer(0, [(y_bank, add_bias_scalar, [0, 1, 2, 3])])
-        pool_in(2, 3)
         own_projection(3)
+        hidden(1, h_banks[1])
+        pool_in(3, 1)
+        pool_in(2, 3)
         pool_in(3, 2)
-        second_layer(1, [(s_banks[0], add_bias_scalar, [0, 1, 2, 3])])
-        turn(2)
+        hidden(2, h_banks[0])
         pool_in(3, 3)
-        turn(3)
-        second_layer(2, [(y_bank, add_bias_scalar, [0, 1, 2, 3])])
-        second_layer(3, [(s_banks[1], add_bias_scalar, [0, 1]), (v_banks[0], add_bias_vector, [2, 3])])
+        hidden(3, h_banks[1])
+        quantize_h(0)
+        quantize_h(1)
+        quantize_h(3)
+        quantize_h(2)
+        second_layer(3, [(v_banks[1], add_bias_scalar, 0, 2), (v_banks[2], add_bias_vector, 2, 4)])
+        second_layer(0, [(s_banks[0], add_bias_scalar, 0, 4)])
+        second_layer(1, [(s_banks[1], add_bias_vector, 0, 4)])
+        second_layer(2, [(v_banks[0], add_bias_scalar, 0, 4)])

@@ -23,6 +23,7 @@ CH = 128
 CHUNKS = J // CH
 HALF = 256
 V_BANKS = 4
+HOLD = 0
 
 
 def tile_list_pnet_bias_kernel(
@@ -55,17 +56,23 @@ def tile_list_pnet_bias_kernel(
             nc.sync.dma_start(raw[:], src.rearrange("(p i) x -> p i x", i=PACK))
             return raw
 
-        wc_raw = [load_rows("wc_raw0", wc[:, 0:HALF])]
         nc.sync.dma_start(tab_codes[:], tab_words[0].rearrange("p t i -> p (t i)").bitcast(I32))
         for q in range(4):
             nc.sync.dma_start(w_plane[32 * q : 32 * q + 4, :], w_scales[0, 4 * q : 4 * q + 4, :].bitcast(I32))
         nc.sync.dma_start(w_codes[:], w_words[0].bitcast(I32))
-        wc_raw.append(load_rows("wc_raw1", wc[:, HALF:R]))
+        wc_raw = [load_rows("wc_raw%d" % u, wc[:, HALF * u : HALF * (u + 1)]) for u in range(2)]
+
+        got_rows = tile("got_rows", [P, G * J], U8)
+        got_plane = tile("got_plane", [P, G * J], U8)
+        nc.vector.tensor_copy(got_rows[:], tab_plane[:].bitcast(U8).indirect(offsets[:]))
+        for q in range(4):
+            rows = slice(P - 16 + 4 * q, P - 16 + 4 * q + 4)
+            nc.sync.dma_start(got_plane[32 * q : 32 * q + 4, :].bitcast(I32), got_rows[rows, :].bitcast(I32))
+
         c_raw = [load_rows("c_raw%d" % u, c[:, HALF * u : HALF * (u + 1)]) for u in range(2)]
         wd_raw = load_rows("wd_raw", wd)
         with nc.allow_non_contiguous_dma(reason="one bias value a partition"):
-            nc.gpsimd.dma_start(bias[:], b.rearrange("(q p) -> p q", p=P))
-
+            nc.sync.dma_start(bias[:], b.rearrange("(q p) -> p q", p=P))
 
         def woven(dst, src):
             return (
@@ -76,15 +83,7 @@ def tile_list_pnet_bias_kernel(
         def quantize(codes, plane, src):
             nc.vector.quantize_mx(out=codes.bitcast(FP8X4), scales=plane, in_=src.rearrange("p x i -> p (x i)"))
 
-        got_rows = tile("got_rows", [P, G * J], U8)
-        got_plane = tile("got_plane", [P, G * J], U8)
         got_codes = [tile("got_codes%d" % g, [P, J], U32) for g in range(G)]
-
-        def gather_scales():
-            nc.vector.tensor_copy(got_rows[:], tab_plane[:].bitcast(U8).indirect(offsets[:]))
-            for q in range(4):
-                rows = slice(P - 16 + 4 * q, P - 16 + 4 * q + 4)
-                nc.scalar.dma_start(got_plane[32 * q : 32 * q + 4, :].bitcast(I32), got_rows[rows, :].bitcast(I32))
 
         def gather_codes(g):
             cols = slice(g * J // 16, (g + 1) * J // 16)
@@ -95,7 +94,7 @@ def tile_list_pnet_bias_kernel(
         h_banks = [ps.tile([P, R], F32, name="h_bank%d" % i) for i in range(2)]
 
         pooled = [
-            c_raw[k // 2][:, 2 * (k % 2) : 2 * (k % 2) + 2, :].rearrange("p a (e q) -> p (a e) q", q=P)
+            (wc_raw[1], c_raw[HOLD])[k // 2][:, 2 * (k % 2) : 2 * (k % 2) + 2, :].rearrange("p a (e q) -> p (a e) q", q=P)
             for k in range(CHUNKS)
         ]
         own = [tile("own%d" % k, [P, PACK, P], F32) for k in range(CHUNKS)]
@@ -126,8 +125,7 @@ def tile_list_pnet_bias_kernel(
                 stop=True,
             )
 
-        def first_neighbour(k):
-            bank = s_banks[k % 2]
+        def first_neighbour(k, bank):
             project(bank, 0, k)
             nc.scalar.copy(pooled[k], dealt(bank))
 
@@ -152,8 +150,7 @@ def tile_list_pnet_bias_kernel(
         def quantize_c(u):
             quantize(c_codes[u][:], c_plane[u][:], c_bf[u][:])
 
-        def own_projection(k):
-            bank = s_banks[k % 2]
+        def own_projection(k, bank):
             cols = slice(CH * (k % 2), CH * (k % 2 + 1))
             nc.tensor.matmul_mx(
                 out=bank[:],
@@ -212,54 +209,57 @@ def tile_list_pnet_bias_kernel(
                 add_bias(result, bank, lo, hi)
                 nc.sync.dma_start(out_rows[:, lo:hi, CH * k : CH * (k + 1)], result[:])
 
-        round_wc(0)
-        gather_scales()
-        quantize_wc(0)
         for g in range(G):
             gather_codes(g)
+        round_wc(0)
         round_wc(1)
+
+        def copy_gpsimd(dst, src):
+            nc.gpsimd.tensor_scalar(dst, src, 1.0, 0.0, ALU.mult, ALU.add)
 
         def round_wd(copy, lo, hi):
             copy(*woven(wd_bf[:, lo:hi, :], wd_raw[:, :, lo:hi]))
 
+        first_neighbour(0, s_banks[0])
+        first_neighbour(1, s_banks[1])
         round_c(0)
-        first_neighbour(0)
-        first_neighbour(1)
+        quantize_wc(0)
         quantize_wc(1)
         quantize_c(0)
-        own_projection(0)
+        first_neighbour(2, h_banks[0])
+        first_neighbour(3, h_banks[1])
+        own_projection(0, s_banks[0])
+        own_projection(1, s_banks[1])
         round_c(1)
-        own_projection(1)
         pool_in(0, 1)
         pool_in(1, 1)
-        first_neighbour(2)
         pool_in(0, 2)
         pool_in(1, 2)
-        first_neighbour(3)
         pool_in(0, 3)
         quantize_c(1)
         pool_in(2, 1)
         round_wd(nc.scalar.copy, 0 * P, 1 * P)
         round_wd(nc.scalar.copy, 1 * P, 2 * P)
-        round_wd(nc.vector.tensor_copy, 2 * P, 4 * P)
-        quantize(wd_codes[:], wd_plane[:], wd_bf[:])
-        own_projection(2)
+        round_wd(nc.scalar.copy, 2 * P, 3 * P)
+        round_wd(nc.vector.tensor_copy, 3 * P, 4 * P)
         hidden(0, h_banks[0])
         pool_in(1, 3)
+        own_projection(2, s_banks[0])
+        quantize(wd_codes[:], wd_plane[:], wd_bf[:])
         pool_in(2, 2)
-        own_projection(3)
+        own_projection(3, s_banks[1])
         hidden(1, h_banks[1])
+        quantize_h(0)
         pool_in(3, 1)
+        second_layer(0, [(s_banks[0], add_bias_scalar, 0, 4)])
         pool_in(2, 3)
+        quantize_h(1)
         pool_in(3, 2)
         hidden(2, h_banks[0])
         pool_in(3, 3)
         hidden(3, h_banks[1])
-        quantize_h(0)
-        quantize_h(1)
         quantize_h(3)
         quantize_h(2)
         second_layer(3, [(v_banks[1], add_bias_scalar, 0, 2), (v_banks[2], add_bias_vector, 2, 4)])
-        second_layer(0, [(s_banks[0], add_bias_scalar, 0, 4)])
         second_layer(1, [(s_banks[1], add_bias_vector, 0, 4)])
         second_layer(2, [(v_banks[0], add_bias_scalar, 0, 4)])

@@ -19,11 +19,15 @@ ACT = mybir.ActivationFunctionType
 
 P = 128
 PACK = 4
-CH = 128
-CHUNKS = J // CH
+QUADRANT = 32
+SCALE_ROWS = K // 32
+PER_COLUMN = 16
+CHUNK = 128
+CHUNKS = J // CHUNK
 HALF = 256
-V_BANKS = 4
-HOLD = 0
+ROW_TILES = N // P
+MAX_BANKS = 4
+WD_TILES_ON_SCALAR = 3
 
 
 def tile_list_pnet_bias_kernel(
@@ -37,68 +41,65 @@ def tile_list_pnet_bias_kernel(
         def tile(name, shape, dtype):
             return sb.tile(shape, dtype, name=name, align_bytes=64)
 
-        offsets = sb.tile([P, G * J // 16], U16, name="offsets")
-        tab_plane = tile("tab_plane", [P, T // 4], I32)
+        offsets = sb.tile([P, G * J // PER_COLUMN], U16, name="offsets")
+        tab_rows = tile("tab_rows", [P, T // 4], I32)
         tab_codes = tile("tab_codes", [P, T], I32)
         w_plane = tile("w_plane", [P, R // 4], I32)
         w_codes = tile("w_codes", [P, R // 2], I32)
-        bias = tile("bias", [P, N // P], F32)
+        bias = tile("bias", [P, ROW_TILES], F32)
         ident = tile("ident", [P, P], F32)
 
         make_identity(nc, ident[:])
-        nc.vector.memset(tab_plane[0 : P - 16, :], 0)
 
+        first_row = P - SCALE_ROWS
+        nc.vector.memset(tab_rows[0:first_row, :], 0)
+        nc.sync.dma_start(tab_rows[first_row:P, :], tab_scales[0].bitcast(I32))
         nc.sync.dma_start(offsets[:], offs)
-        nc.sync.dma_start(tab_plane[P - 16 : P, :], tab_scales[0].bitcast(I32))
 
         def load_rows(name, src):
             raw = tile(name, [P, PACK, src.shape[1]], F32)
             nc.sync.dma_start(raw[:], src.rearrange("(p i) x -> p i x", i=PACK))
             return raw
 
+        def plane_rows(q):
+            return slice(QUADRANT * q, QUADRANT * q + 4)
+
         nc.sync.dma_start(tab_codes[:], tab_words[0].rearrange("p t i -> p (t i)").bitcast(I32))
         for q in range(4):
-            nc.sync.dma_start(w_plane[32 * q : 32 * q + 4, :], w_scales[0, 4 * q : 4 * q + 4, :].bitcast(I32))
+            nc.sync.dma_start(w_plane[plane_rows(q), :], w_scales[0, 4 * q : 4 * q + 4, :].bitcast(I32))
         nc.sync.dma_start(w_codes[:], w_words[0].bitcast(I32))
         wc_raw = [load_rows("wc_raw%d" % u, wc[:, HALF * u : HALF * (u + 1)]) for u in range(2)]
 
         got_rows = tile("got_rows", [P, G * J], U8)
         got_plane = tile("got_plane", [P, G * J], U8)
-        nc.vector.tensor_copy(got_rows[:], tab_plane[:].bitcast(U8).indirect(offsets[:]))
+        nc.vector.tensor_copy(got_rows[:], tab_rows[:].bitcast(U8).indirect(offsets[:]))
         for q in range(4):
-            rows = slice(P - 16 + 4 * q, P - 16 + 4 * q + 4)
-            nc.sync.dma_start(got_plane[32 * q : 32 * q + 4, :].bitcast(I32), got_rows[rows, :].bitcast(I32))
+            rows = slice(first_row + 4 * q, first_row + 4 * q + 4)
+            nc.sync.dma_start(got_plane[plane_rows(q), :].bitcast(I32), got_rows[rows, :].bitcast(I32))
 
         c_raw = [load_rows("c_raw%d" % u, c[:, HALF * u : HALF * (u + 1)]) for u in range(2)]
         wd_raw = load_rows("wd_raw", wd)
-        with nc.allow_non_contiguous_dma(reason="one bias value a partition"):
+        with nc.allow_non_contiguous_dma(reason="one bias value a partition and row tile"):
             nc.sync.dma_start(bias[:], b.rearrange("(q p) -> p q", p=P))
 
-        def woven(dst, src):
-            return (
-                dst.rearrange("p (x u) i -> p x i u", u=4),
-                src.rearrange("p i (x u) -> p x i u", u=4),
-            )
+        def round_and_weave(copy, dst, src):
+            copy(dst.rearrange("p (x u) i -> p x i u", u=4), src.rearrange("p i (x u) -> p x i u", u=4))
 
         def quantize(codes, plane, src):
             nc.vector.quantize_mx(out=codes.bitcast(FP8X4), scales=plane, in_=src.rearrange("p x i -> p (x i)"))
 
-        got_codes = [tile("got_codes%d" % g, [P, J], U32) for g in range(G)]
-
-        def gather_codes(g):
-            cols = slice(g * J // 16, (g + 1) * J // 16)
-            nc.vector.tensor_copy(got_codes[g][:], tab_codes[:].bitcast(U32).indirect(offsets[:, cols]))
+        got_codes = tile("got_codes", [P, G * J], U32)
 
         s_banks = [ps.tile([P, R], F32, name="s_bank%d" % i) for i in range(2)]
-        v_banks = [ps.tile([P, R], F32, name="v_bank%d" % i) for i in range(V_BANKS)]
+        v_banks = [ps.tile([P, R], F32, name="v_bank%d" % i) for i in range(MAX_BANKS)]
         h_banks = [ps.tile([P, R], F32, name="h_bank%d" % i) for i in range(2)]
 
         pooled = [
-            (wc_raw[1], c_raw[HOLD])[k // 2][:, 2 * (k % 2) : 2 * (k % 2) + 2, :].rearrange("p a (e q) -> p (a e) q", q=P)
+            (wc_raw[1], c_raw[0])[k // 2][:, 2 * (k % 2) : 2 * (k % 2) + 2, :].rearrange("p a (e q) -> p (a e) q", q=P)
             for k in range(CHUNKS)
         ]
         own = [tile("own%d" % k, [P, PACK, P], F32) for k in range(CHUNKS)]
-        wc_bf = [tile("wc_bf%d" % u, [P, HALF, PACK], BF16) for u in range(2)]
+        wc_bf = tile("wc_bf", [P, R, PACK], BF16)
         c_bf = [tile("c_bf%d" % u, [P, HALF, PACK], BF16) for u in range(2)]
         wd_bf = tile("wd_bf", [P, N, PACK], BF16)
         wc_codes = tile("wc_codes", [P, R], U32)
@@ -107,18 +108,19 @@ def tile_list_pnet_bias_kernel(
         c_plane = [tile("c_plane%d" % u, [P, HALF], U8) for u in range(2)]
         wd_codes = tile("wd_codes", [P, N], U32)
         wd_plane = tile("wd_plane", [P, N], U8)
-        h_bf = [tile("h_bf%d" % k, [P, CH, PACK], BF16) for k in range(CHUNKS)]
-        h_codes = [tile("h_codes%d" % k, [P, CH], U32) for k in range(CHUNKS)]
-        h_plane = [tile("h_plane%d" % k, [P, CH], U8) for k in range(CHUNKS)]
+        h_bf = [tile("h_bf%d" % k, [P, CHUNK, PACK], BF16) for k in range(CHUNKS)]
+        h_codes = [tile("h_codes%d" % k, [P, CHUNK], U32) for k in range(CHUNKS)]
+        h_plane = [tile("h_plane%d" % k, [P, CHUNK], U8) for k in range(CHUNKS)]
 
         def dealt(bank):
-            return bank[:].rearrange("p (q t) -> p t q", t=PACK)
+            return bank[:].rearrange("j (p t) -> j t p", t=PACK)
 
         def project(bank, g, k):
+            cols = slice(J * g + CHUNK * k, J * g + CHUNK * (k + 1))
             nc.tensor.matmul_mx(
                 out=bank[:],
-                lhsT=got_codes[g][:, CH * k : CH * (k + 1)].bitcast(FP8X4),
-                lhsT_scale=got_plane[:, J * g + CH * k : J * g + CH * (k + 1)],
+                lhsT=got_codes[:, cols].bitcast(FP8X4),
+                lhsT_scale=got_plane[:, cols],
                 rhs=w_codes[:].bitcast(U8).bitcast(FP4X4),
                 rhs_scale=w_plane[:].bitcast(U8),
                 start=True,
@@ -129,29 +131,28 @@ def tile_list_pnet_bias_kernel(
             project(bank, 0, k)
             nc.scalar.copy(pooled[k], dealt(bank))
 
-        turns = []
+        maxima_done = []
 
         def pool_in(k, g):
-            bank = v_banks[len(turns) % V_BANKS]
-            turns.append((k, g))
+            bank = v_banks[len(maxima_done) % MAX_BANKS]
+            maxima_done.append((k, g))
             project(bank, g, k)
             nc.vector.tensor_tensor(pooled[k], dealt(bank), pooled[k], ALU.max)
 
-        def round_wc(u):
-            nc.scalar.copy(*woven(wc_bf[u][:], wc_raw[u][:]))
-
-        def quantize_wc(u):
-            cols = slice(HALF * u, HALF * (u + 1))
-            quantize(wc_codes[:, cols], wc_plane[:, cols], wc_bf[u][:])
-
         def round_c(u):
-            nc.scalar.copy(*woven(c_bf[u][:], c_raw[u][:]))
+            round_and_weave(nc.scalar.copy, c_bf[u][:], c_raw[u][:])
 
         def quantize_c(u):
             quantize(c_codes[u][:], c_plane[u][:], c_bf[u][:])
 
+        def round_wd():
+            for q in range(ROW_TILES):
+                copy = nc.scalar.copy if q < WD_TILES_ON_SCALAR else nc.vector.tensor_copy
+                cols = slice(P * q, P * (q + 1))
+                round_and_weave(copy, wd_bf[:, cols, :], wd_raw[:, :, cols])
+
         def own_projection(k, bank):
-            cols = slice(CH * (k % 2), CH * (k % 2 + 1))
+            cols = slice(CHUNK * (k % 2), CHUNK * (k % 2 + 1))
             nc.tensor.matmul_mx(
                 out=bank[:],
                 lhsT=c_codes[k // 2][:, cols].bitcast(FP8X4),
@@ -163,85 +164,76 @@ def tile_list_pnet_bias_kernel(
             )
             nc.scalar.copy(own[k][:], dealt(bank))
 
-        def turn(bank, src, opens):
-            for t in range(PACK):
-                nc.tensor.matmul(
-                    bank[:, CH * t : CH * (t + 1)], src[:, t, :], ident[:], is_transpose=True,
-                    start=(opens and t == 0), stop=(not opens and t == PACK - 1),
-                )
-
         def hidden(k, bank):
-            turn(bank, own[k], True)
-            turn(bank, pooled[k], False)
+            for s, src in enumerate((own[k], pooled[k])):
+                for t in range(PACK):
+                    nc.tensor.matmul(
+                        bank[:, CHUNK * t : CHUNK * (t + 1)],
+                        src[:, t, :],
+                        ident[:],
+                        is_transpose=True,
+                        start=(s == 0 and t == 0),
+                        stop=(s == 1 and t == PACK - 1),
+                    )
             nc.scalar.activation(h_bf[k][:], bank[:].rearrange("p (t j) -> p j t", t=PACK), ACT.Relu)
-
-        out_rows = out.rearrange("(q p) j -> p q j", p=P)
-
-        def output_rows(k, bank, q):
-            cols = slice(P * q, P * (q + 1))
-            nc.tensor.matmul_mx(
-                out=bank[:, CH * q : CH * (q + 1)],
-                lhsT=wd_codes[:, cols].bitcast(FP8X4),
-                lhsT_scale=wd_plane[:, cols],
-                rhs=h_codes[k][:].bitcast(FP8X4),
-                rhs_scale=h_plane[k][:],
-                start=True,
-                stop=True,
-            )
-
-        def add_bias_scalar(dst, bank, lo, hi):
-            for q in range(lo, hi):
-                nc.scalar.activation(dst[:, q - lo, :], bank[:, CH * q : CH * (q + 1)], ACT.Identity, bias=bias[:, q : q + 1])
-
-        def add_bias_vector(dst, bank, lo, hi):
-            sums = bank[:, CH * lo : CH * hi].rearrange("p (q j) -> p q j", j=CH)
-            nc.vector.tensor_tensor(dst[:], sums, bias[:, lo:hi].unsqueeze(2).to_broadcast([P, hi - lo, CH]), ALU.add)
 
         def quantize_h(k):
             quantize(h_codes[k][:], h_plane[k][:], h_bf[k][:])
 
+        out_rows = out.rearrange("(q p) j -> p q j", p=P)
+
+        def add_bias_scalar(dst, bank, lo, hi):
+            for q in range(lo, hi):
+                sums = bank[:, CHUNK * q : CHUNK * (q + 1)]
+                nc.scalar.activation(dst[:, q - lo, :], sums, ACT.Identity, bias=bias[:, q : q + 1])
+
+        def add_bias_vector(dst, bank, lo, hi):
+            sums = bank[:, CHUNK * lo : CHUNK * hi].rearrange("p (q j) -> p q j", j=CHUNK)
+            nc.vector.tensor_tensor(dst[:], sums, bias[:, lo:hi].unsqueeze(2).to_broadcast([P, hi - lo, CHUNK]), ALU.add)
+
         def second_layer(k, shares):
-            for bank, add_bias, lo, hi in shares:
+            for bank, add_bias, queue, lo, hi in shares:
                 for q in range(lo, hi):
-                    output_rows(k, bank, q)
-            for bank, add_bias, lo, hi in shares:
-                result = tile("result%d_%d" % (k, lo), [P, hi - lo, CH], F32)
+                    cols = slice(P * q, P * (q + 1))
+                    nc.tensor.matmul_mx(
+                        out=bank[:, CHUNK * q : CHUNK * (q + 1)],
+                        lhsT=wd_codes[:, cols].bitcast(FP8X4),
+                        lhsT_scale=wd_plane[:, cols],
+                        rhs=h_codes[k][:].bitcast(FP8X4),
+                        rhs_scale=h_plane[k][:],
+                        start=True,
+                        stop=True,
+                    )
+            for bank, add_bias, queue, lo, hi in shares:
+                result = tile("result%d_%d" % (k, lo), [P, hi - lo, CHUNK], F32)
                 add_bias(result, bank, lo, hi)
-                nc.sync.dma_start(out_rows[:, lo:hi, CH * k : CH * (k + 1)], result[:])
+                queue.dma_start(out_rows[:, lo:hi, CHUNK * k : CHUNK * (k + 1)], result[:])
 
-        for g in range(G):
-            gather_codes(g)
-        round_wc(0)
-        round_wc(1)
-
-        def copy_gpsimd(dst, src):
-            nc.gpsimd.tensor_scalar(dst, src, 1.0, 0.0, ALU.mult, ALU.add)
-
-        def round_wd(copy, lo, hi):
-            copy(*woven(wd_bf[:, lo:hi, :], wd_raw[:, :, lo:hi]))
+        for u in range(2):
+            list_cols = slice(u * 2 * J // PER_COLUMN, (u + 1) * 2 * J // PER_COLUMN)
+            picked = tab_codes[:].bitcast(U32).indirect(offsets[:, list_cols])
+            nc.vector.tensor_copy(got_codes[:, u * 2 * J : (u + 1) * 2 * J], picked)
+        for u in range(2):
+            round_and_weave(nc.scalar.copy, wc_bf[:, HALF * u : HALF * (u + 1), :], wc_raw[u][:])
 
         first_neighbour(0, s_banks[0])
         first_neighbour(1, s_banks[1])
         round_c(0)
-        quantize_wc(0)
-        quantize_wc(1)
+        quantize(wc_codes[:], wc_plane[:], wc_bf[:])
         quantize_c(0)
+        pool_in(0, 1)
+        pool_in(1, 1)
         first_neighbour(2, h_banks[0])
         first_neighbour(3, h_banks[1])
         own_projection(0, s_banks[0])
         own_projection(1, s_banks[1])
         round_c(1)
-        pool_in(0, 1)
-        pool_in(1, 1)
         pool_in(0, 2)
         pool_in(1, 2)
         pool_in(0, 3)
         quantize_c(1)
         pool_in(2, 1)
-        round_wd(nc.scalar.copy, 0 * P, 1 * P)
-        round_wd(nc.scalar.copy, 1 * P, 2 * P)
-        round_wd(nc.scalar.copy, 2 * P, 3 * P)
-        round_wd(nc.vector.tensor_copy, 3 * P, 4 * P)
+        round_wd()
         hidden(0, h_banks[0])
         pool_in(1, 3)
         own_projection(2, s_banks[0])
@@ -251,15 +243,20 @@ def tile_list_pnet_bias_kernel(
         hidden(1, h_banks[1])
         quantize_h(0)
         pool_in(3, 1)
-        second_layer(0, [(s_banks[0], add_bias_scalar, 0, 4)])
+        second_layer(0, [(s_banks[0], add_bias_scalar, nc.sync, 0, ROW_TILES)])
         pool_in(2, 3)
         quantize_h(1)
         pool_in(3, 2)
         hidden(2, h_banks[0])
         pool_in(3, 3)
         hidden(3, h_banks[1])
+
         quantize_h(3)
         quantize_h(2)
-        second_layer(3, [(v_banks[1], add_bias_scalar, 0, 2), (v_banks[2], add_bias_vector, 2, 4)])
-        second_layer(1, [(s_banks[1], add_bias_vector, 0, 4)])
-        second_layer(2, [(v_banks[0], add_bias_scalar, 0, 4)])
+        middle = ROW_TILES // 2
+        second_layer(
+            3,
+            [(v_banks[1], add_bias_scalar, nc.scalar, 0, middle), (v_banks[2], add_bias_vector, nc.sync, middle, ROW_TILES)],
+        )
+        second_layer(1, [(s_banks[1], add_bias_vector, nc.sync, 0, ROW_TILES)])
+        second_layer(2, [(v_banks[0], add_bias_scalar, nc.sync, 0, ROW_TILES)])

@@ -27,7 +27,6 @@ CHUNKS = J // CHUNK
 HALF = 256
 ROW_TILES = N // P
 MAX_BANKS = 4
-WD_TILES_ON_SCALAR = 3
 
 
 def tile_list_pnet_bias_kernel(
@@ -48,9 +47,11 @@ def tile_list_pnet_bias_kernel(
         w_codes = tile("w_codes", [P, R // 2], I32)
         bias = tile("bias", [P, ROW_TILES], F32)
         ident = tile("ident", [P, P], F32)
+        got_rows = tile("got_rows", [P, G * J], U8)
+        got_plane = tile("got_plane", [P, G * J], U8)
+        got_codes = tile("got_codes", [P, G * J], U32)
 
         make_identity(nc, ident[:])
-
         first_row = P - SCALE_ROWS
         nc.vector.memset(tab_rows[0:first_row, :], 0)
         nc.sync.dma_start(tab_rows[first_row:P, :], tab_scales[0].bitcast(I32))
@@ -61,59 +62,86 @@ def tile_list_pnet_bias_kernel(
             nc.sync.dma_start(raw[:], src.rearrange("(p i) x -> p i x", i=PACK))
             return raw
 
-        def plane_rows(q):
-            return slice(QUADRANT * q, QUADRANT * q + 4)
+        def plane_rows(r):
+            return slice(r, P, QUADRANT)
 
-        nc.sync.dma_start(tab_codes[:], tab_words[0].rearrange("p t i -> p (t i)").bitcast(I32))
-        for q in range(4):
-            nc.sync.dma_start(w_plane[plane_rows(q), :], w_scales[0, 4 * q : 4 * q + 4, :].bitcast(I32))
-        nc.sync.dma_start(w_codes[:], w_words[0].bitcast(I32))
-        wc_raw = [load_rows("wc_raw%d" % u, wc[:, HALF * u : HALF * (u + 1)]) for u in range(2)]
+        def load_words():
+            nc.sync.dma_start(tab_codes[:], tab_words[0].rearrange("p t i -> p (t i)").bitcast(I32))
 
-        got_rows = tile("got_rows", [P, G * J], U8)
-        got_plane = tile("got_plane", [P, G * J], U8)
-        nc.vector.tensor_copy(got_rows[:], tab_rows[:].bitcast(U8).indirect(offsets[:]))
-        for q in range(4):
-            rows = slice(first_row + 4 * q, first_row + 4 * q + 4)
-            nc.sync.dma_start(got_plane[plane_rows(q), :].bitcast(I32), got_rows[rows, :].bitcast(I32))
+        def load_w_plane():
+            for r in range(4):
+                nc.sync.dma_start(w_plane[plane_rows(r), :], w_scales[0, r:SCALE_ROWS:4, :].bitcast(I32))
 
-        c_raw = [load_rows("c_raw%d" % u, c[:, HALF * u : HALF * (u + 1)]) for u in range(2)]
+        def load_w_codes():
+            nc.sync.dma_start(w_codes[:], w_words[0].bitcast(I32))
+
+        def gather_scales():
+            nc.vector.tensor_copy(got_rows[:], tab_rows[:].bitcast(U8).indirect(offsets[:]))
+
+        def move_scales(queue):
+            for r in range(4):
+                rows = slice(first_row + r, P, 4)
+                queue.dma_start(got_plane[plane_rows(r), :].bitcast(I32), got_rows[rows, :].bitcast(I32))
+
+        def load_bias():
+            with nc.allow_non_contiguous_dma(reason="one bias value a partition and row tile"):
+                nc.sync.dma_start(bias[:], b.rearrange("(q p) -> p q", p=P))
+
+        nc.vector.memset(w_plane[:], 0)
+        load_words()
+        load_w_plane()
+        load_w_codes()
+        wc_raw = [load_rows("wc_raw0", wc[:, 0:HALF])]
+        gather_scales()
+        move_scales(nc.sync)
+        wc_raw.append(load_rows("wc_raw1", wc[:, HALF:R]))
+        c_raw = load_rows("c_raw", c)
         wd_raw = load_rows("wd_raw", wd)
-        with nc.allow_non_contiguous_dma(reason="one bias value a partition and row tile"):
-            nc.sync.dma_start(bias[:], b.rearrange("(q p) -> p q", p=P))
+        load_bias()
 
-        def round_and_weave(copy, dst, src):
+        def weave(copy, dst, src):
             copy(dst.rearrange("p (x u) i -> p x i u", u=4), src.rearrange("p i (x u) -> p x i u", u=4))
+
+        def on_gpsimd(dst, src):
+            nc.gpsimd.tensor_scalar(dst, src.rearrange("p i x -> p x i"), 1.0, 0.0, ALU.mult, ALU.add)
+
+        def on_scalar(dst, src):
+            weave(nc.scalar.copy, dst, src)
+
+        def on_vector(dst, src):
+            weave(nc.vector.tensor_copy, dst, src)
 
         def quantize(codes, plane, src):
             nc.vector.quantize_mx(out=codes.bitcast(FP8X4), scales=plane, in_=src.rearrange("p x i -> p (x i)"))
 
-        got_codes = tile("got_codes", [P, G * J], U32)
+        banks = [ps.tile([P, R], F32, name="bank%d" % i) for i in range(8)]
+        s_banks, v_banks, h_banks = banks[0:2], banks[2:6], banks[6:8]
 
-        s_banks = [ps.tile([P, R], F32, name="s_bank%d" % i) for i in range(2)]
-        v_banks = [ps.tile([P, R], F32, name="v_bank%d" % i) for i in range(MAX_BANKS)]
-        h_banks = [ps.tile([P, R], F32, name="h_bank%d" % i) for i in range(2)]
-
-        pooled = [
-            (wc_raw[1], c_raw[0])[k // 2][:, 2 * (k % 2) : 2 * (k % 2) + 2, :].rearrange("p a (e q) -> p (a e) q", q=P)
-            for k in range(CHUNKS)
-        ]
+        pooled = [tile("pooled%d" % k, [P, PACK, P], F32)[:] for k in range(CHUNKS)]
         own = [tile("own%d" % k, [P, PACK, P], F32) for k in range(CHUNKS)]
         wc_bf = tile("wc_bf", [P, R, PACK], BF16)
-        c_bf = [tile("c_bf%d" % u, [P, HALF, PACK], BF16) for u in range(2)]
+        c_bf = tile("c_bf", [P, J, PACK], BF16)
         wd_bf = tile("wd_bf", [P, N, PACK], BF16)
         wc_codes = tile("wc_codes", [P, R], U32)
         wc_plane = tile("wc_plane", [P, R], U8)
-        c_codes = [tile("c_codes%d" % u, [P, HALF], U32) for u in range(2)]
-        c_plane = [tile("c_plane%d" % u, [P, HALF], U8) for u in range(2)]
+        c_codes = tile("c_codes", [P, J], U32)
+        c_plane = tile("c_plane", [P, J], U8)
         wd_codes = tile("wd_codes", [P, N], U32)
         wd_plane = tile("wd_plane", [P, N], U8)
-        h_bf = [tile("h_bf%d" % k, [P, CHUNK, PACK], BF16) for k in range(CHUNKS)]
-        h_codes = [tile("h_codes%d" % k, [P, CHUNK], U32) for k in range(CHUNKS)]
-        h_plane = [tile("h_plane%d" % k, [P, CHUNK], U8) for k in range(CHUNKS)]
+        h_bf = tile("h_bf", [P, J, PACK], BF16)
+        h_codes = tile("h_codes", [P, J], U32)
+        h_plane = tile("h_plane", [P, J], U8)
+
+        def points(k, count=1):
+            return slice(CHUNK * k, CHUNK * (k + count))
 
         def dealt(bank):
             return bank[:].rearrange("j (p t) -> j t p", t=PACK)
+
+        def gather_words(g, count):
+            list_cols = slice(g * J // PER_COLUMN, (g + count) * J // PER_COLUMN)
+            picked = tab_codes[:].bitcast(U32).indirect(offsets[:, list_cols])
+            nc.vector.tensor_copy(got_codes[:, g * J : (g + count) * J], picked)
 
         def project(bank, g, k):
             cols = slice(J * g + CHUNK * k, J * g + CHUNK * (k + 1))
@@ -127,36 +155,41 @@ def tile_list_pnet_bias_kernel(
                 stop=True,
             )
 
+        def to_sbuf(dst, k, g, bank):
+            project(bank, g, k)
+            nc.scalar.copy(dst, dealt(bank))
+
         def first_neighbour(k, bank):
-            project(bank, 0, k)
-            nc.scalar.copy(pooled[k], dealt(bank))
+            to_sbuf(pooled[k], k, 0, bank)
 
         maxima_done = []
 
-        def pool_in(k, g):
+        def pool_in(k, g, dst=None):
+            dst = pooled[k] if dst is None else dst
             bank = v_banks[len(maxima_done) % MAX_BANKS]
             maxima_done.append((k, g))
             project(bank, g, k)
-            nc.vector.tensor_tensor(pooled[k], dealt(bank), pooled[k], ALU.max)
+            nc.vector.tensor_tensor(dst, dealt(bank), dst, ALU.max)
 
-        def round_c(u):
-            round_and_weave(nc.scalar.copy, c_bf[u][:], c_raw[u][:])
+        def quantize_wc():
+            quantize(wc_codes[:], wc_plane[:], wc_bf[:])
 
-        def quantize_c(u):
-            quantize(c_codes[u][:], c_plane[u][:], c_bf[u][:])
+        def quantize_wd():
+            quantize(wd_codes[:], wd_plane[:], wd_bf[:])
 
-        def round_wd():
-            for q in range(ROW_TILES):
-                copy = nc.scalar.copy if q < WD_TILES_ON_SCALAR else nc.vector.tensor_copy
-                cols = slice(P * q, P * (q + 1))
-                round_and_weave(copy, wd_bf[:, cols, :], wd_raw[:, :, cols])
+        def quantize_c(k, count):
+            cols = points(k, count)
+            quantize(c_codes[:, cols], c_plane[:, cols], c_bf[:, cols, :])
+
+        def quantize_h(k, count=1):
+            cols = points(k, count)
+            quantize(h_codes[:, cols], h_plane[:, cols], h_bf[:, cols, :])
 
         def own_projection(k, bank):
-            cols = slice(CHUNK * (k % 2), CHUNK * (k % 2 + 1))
             nc.tensor.matmul_mx(
                 out=bank[:],
-                lhsT=c_codes[k // 2][:, cols].bitcast(FP8X4),
-                lhsT_scale=c_plane[k // 2][:, cols],
+                lhsT=c_codes[:, points(k)].bitcast(FP8X4),
+                lhsT_scale=c_plane[:, points(k)],
                 rhs=wc_codes[:].bitcast(FP8X4),
                 rhs_scale=wc_plane[:],
                 start=True,
@@ -164,8 +197,8 @@ def tile_list_pnet_bias_kernel(
             )
             nc.scalar.copy(own[k][:], dealt(bank))
 
-        def hidden(k, bank):
-            for s, src in enumerate((own[k], pooled[k])):
+        def turn(bank, first, second):
+            for s, src in enumerate((first, second)):
                 for t in range(PACK):
                     nc.tensor.matmul(
                         bank[:, CHUNK * t : CHUNK * (t + 1)],
@@ -175,88 +208,155 @@ def tile_list_pnet_bias_kernel(
                         start=(s == 0 and t == 0),
                         stop=(s == 1 and t == PACK - 1),
                     )
-            nc.scalar.activation(h_bf[k][:], bank[:].rearrange("p (t j) -> p j t", t=PACK), ACT.Relu)
+            return bank[:].rearrange("p (t j) -> p j t", t=PACK)
 
-        def quantize_h(k):
-            quantize(h_codes[k][:], h_plane[k][:], h_bf[k][:])
+        def hidden(k, bank):
+            nc.scalar.activation(h_bf[:, points(k), :], turn(bank, own[k], pooled[k]), ACT.Relu)
 
         out_rows = out.rearrange("(q p) j -> p q j", p=P)
 
-        def add_bias_scalar(dst, bank, lo, hi):
+        def add_bias_scalar(dst, sums, lo, hi):
             for q in range(lo, hi):
-                sums = bank[:, CHUNK * q : CHUNK * (q + 1)]
-                nc.scalar.activation(dst[:, q - lo, :], sums, ACT.Identity, bias=bias[:, q : q + 1])
+                nc.scalar.activation(dst[:, q - lo, :], sums[:, q - lo, :], ACT.Identity, bias=bias[:, q : q + 1])
 
-        def add_bias_vector(dst, bank, lo, hi):
-            sums = bank[:, CHUNK * lo : CHUNK * hi].rearrange("p (q j) -> p q j", j=CHUNK)
-            nc.vector.tensor_tensor(dst[:], sums, bias[:, lo:hi].unsqueeze(2).to_broadcast([P, hi - lo, CHUNK]), ALU.add)
+        def add_bias_vector(dst, sums, lo, hi):
+            nc.vector.tensor_tensor(dst[:], sums, bias[:, lo:hi].unsqueeze(2).to_broadcast(list(sums.shape)), ALU.add)
 
-        def second_layer(k, shares):
+        def second_layer(k, count, shares):
+            width = CHUNK * count
+            cols = points(k, count)
             for bank, add_bias, queue, lo, hi in shares:
                 for q in range(lo, hi):
-                    cols = slice(P * q, P * (q + 1))
                     nc.tensor.matmul_mx(
-                        out=bank[:, CHUNK * q : CHUNK * (q + 1)],
-                        lhsT=wd_codes[:, cols].bitcast(FP8X4),
-                        lhsT_scale=wd_plane[:, cols],
-                        rhs=h_codes[k][:].bitcast(FP8X4),
-                        rhs_scale=h_plane[k][:],
+                        out=bank[:, width * (q - lo) : width * (q - lo + 1)],
+                        lhsT=wd_codes[:, P * q : P * (q + 1)].bitcast(FP8X4),
+                        lhsT_scale=wd_plane[:, P * q : P * (q + 1)],
+                        rhs=h_codes[:, cols].bitcast(FP8X4),
+                        rhs_scale=h_plane[:, cols],
                         start=True,
                         stop=True,
                     )
             for bank, add_bias, queue, lo, hi in shares:
-                result = tile("result%d_%d" % (k, lo), [P, hi - lo, CHUNK], F32)
-                add_bias(result, bank, lo, hi)
-                queue.dma_start(out_rows[:, lo:hi, CHUNK * k : CHUNK * (k + 1)], result[:])
+                result = tile("result%d_%d" % (k, lo), [P, hi - lo, width], F32)
+                sums = bank[:, 0 : width * (hi - lo)].rearrange("p (q j) -> p q j", j=width)
+                add_bias(result, sums, lo, hi)
+                queue.dma_start(out_rows[:, lo:hi, cols], result[:])
 
-        for u in range(2):
-            list_cols = slice(u * 2 * J // PER_COLUMN, (u + 1) * 2 * J // PER_COLUMN)
-            picked = tab_codes[:].bitcast(U32).indirect(offsets[:, list_cols])
-            nc.vector.tensor_copy(got_codes[:, u * 2 * J : (u + 1) * 2 * J], picked)
-        for u in range(2):
-            round_and_weave(nc.scalar.copy, wc_bf[:, HALF * u : HALF * (u + 1), :], wc_raw[u][:])
+        w_dealt = tile("w_dealt", [P, PACK, P, 2], U8)
+        w_plane_dealt = tile("w_plane_dealt", [P, PACK, P], U8)
 
+        def deal_w():
+            nc.gpsimd.tensor_copy(w_dealt[:], w_codes[:].bitcast(U8).rearrange("p (m t e) -> p t m e", t=PACK, e=2))
+            nc.gpsimd.tensor_copy(w_plane_dealt[:], w_plane[:].bitcast(U8).rearrange("p (m t) -> p t m", t=PACK))
+
+        def round_wc(u):
+            dst = wc_bf[:].rearrange("p (t m) i -> p m i t", t=PACK)[:, HALF // PACK * u : HALF // PACK * (u + 1), :, :]
+            nc.scalar.copy(dst, wc_raw[u][:].rearrange("p i (m t) -> p m i t", t=PACK))
+
+        def cast(on, dst, src, lo, hi):
+            on(dst[:, P * lo : P * hi, :], src[:, :, P * lo : P * hi])
+
+        def own_turned(k, bank):
+            nc.tensor.matmul_mx(
+                out=bank[:],
+                lhsT=c_codes[:, points(k)].bitcast(FP8X4),
+                lhsT_scale=c_plane[:, points(k)],
+                rhs=wc_codes[:].bitcast(FP8X4),
+                rhs_scale=wc_plane[:],
+                start=True,
+                stop=True,
+            )
+            nc.scalar.copy(own[k][:], bank[:].rearrange("j (t m) -> j t m", t=PACK))
+
+        def rows_product(bank, k, g, with_own):
+            for t in range(PACK):
+                dst = bank[:, CHUNK * t : CHUNK * (t + 1)]
+                if g is not None:
+                    cols = slice(J * g + CHUNK * k, J * g + CHUNK * (k + 1))
+                    nc.tensor.matmul_mx(
+                        out=dst,
+                        lhsT=w_dealt[:, t, :, :].rearrange("p m e -> p (m e)").bitcast(FP4X4),
+                        lhsT_scale=w_plane_dealt[:, t, :],
+                        rhs=got_codes[:, cols].bitcast(FP8X4),
+                        rhs_scale=got_plane[:, cols],
+                        start=True,
+                        stop=not with_own,
+                    )
+                if with_own:
+                    nc.tensor.matmul_mx(
+                        out=dst,
+                        lhsT=wc_codes[:, P * t : P * (t + 1)].bitcast(FP8X4),
+                        lhsT_scale=wc_plane[:, P * t : P * (t + 1)],
+                        rhs=c_codes[:, points(k)].bitcast(FP8X4),
+                        rhs_scale=c_plane[:, points(k)],
+                        start=g is None,
+                        stop=True,
+                    )
+            return bank[:].rearrange("p (t j) -> p j t", t=PACK)
+
+        def woven(k):
+            return pooled[k].rearrange("p a b -> p (a b)").rearrange("p (j t) -> p j t", t=PACK)
+
+        def take_bank():
+            maxima_done.append(None)
+            return v_banks[(len(maxima_done) - 1) % MAX_BANKS]
+
+        def rows_first(k, bank):
+            nc.scalar.copy(woven(k), rows_product(bank, k, 0, False))
+
+        def rows_pool_in(k, g):
+            nc.vector.tensor_tensor(woven(k), rows_product(take_bank(), k, g, False), woven(k), ALU.max)
+
+        def rows_add_own(k, sums):
+            nc.vector.tensor_tensor(woven(k), sums, woven(k), ALU.add)
+
+        def rows_last(k, sums):
+            nc.vector.scalar_tensor_tensor(h_bf[:, points(k), :], sums, 0.0, woven(k), ALU.max, ALU.max)
+
+        gather_words(0, 2)
+        gather_words(2, 2)
+        deal_w()
+        round_wc(0)
         first_neighbour(0, s_banks[0])
         first_neighbour(1, s_banks[1])
-        round_c(0)
-        quantize(wc_codes[:], wc_plane[:], wc_bf[:])
-        quantize_c(0)
+        round_wc(1)
         pool_in(0, 1)
         pool_in(1, 1)
-        first_neighbour(2, h_banks[0])
-        first_neighbour(3, h_banks[1])
-        own_projection(0, s_banks[0])
-        own_projection(1, s_banks[1])
-        round_c(1)
+        cast(on_scalar, c_bf, c_raw, 0, 2)
+        quantize_wc()
+        quantize_c(0, 2)
+        own_turned(0, s_banks[0])
+        own_turned(1, s_banks[1])
+        rows_first(2, h_banks[0])
+        rows_first(3, h_banks[1])
+        cast(on_scalar, c_bf, c_raw, 2, 4)
         pool_in(0, 2)
         pool_in(1, 2)
         pool_in(0, 3)
-        quantize_c(1)
-        pool_in(2, 1)
-        round_wd()
-        hidden(0, h_banks[0])
         pool_in(1, 3)
-        own_projection(2, s_banks[0])
-        quantize(wd_codes[:], wd_plane[:], wd_bf[:])
-        pool_in(2, 2)
-        own_projection(3, s_banks[1])
+        quantize_c(2, 2)
+        rows_pool_in(2, 1)
+        rows_pool_in(3, 1)
+        rows_pool_in(2, 2)
+        rows_pool_in(3, 2)
+        own2 = rows_product(s_banks[0], 2, None, True)
+        hidden(0, h_banks[0])
+        own3 = rows_product(s_banks[1], 3, None, True)
+        last2 = rows_product(v_banks[2], 2, 3, True)
         hidden(1, h_banks[1])
+        cast(on_scalar, wd_bf, wd_raw, 0, 2)
+        cast(on_vector, wd_bf, wd_raw, 2, 4)
+        quantize_wd()
         quantize_h(0)
-        pool_in(3, 1)
-        second_layer(0, [(s_banks[0], add_bias_scalar, nc.sync, 0, ROW_TILES)])
-        pool_in(2, 3)
+        second_layer(0, 1, [(v_banks[0], add_bias_scalar, nc.sync, 0, 4)])
+        last3 = rows_product(v_banks[3], 3, 3, True)
+        rows_add_own(2, own2)
         quantize_h(1)
-        pool_in(3, 2)
-        hidden(2, h_banks[0])
-        pool_in(3, 3)
-        hidden(3, h_banks[1])
-
-        quantize_h(3)
+        second_layer(1, 1, [(v_banks[1], add_bias_scalar, nc.sync, 0, 4)])
+        rows_last(2, last2)
+        rows_add_own(3, own3)
         quantize_h(2)
-        middle = ROW_TILES // 2
-        second_layer(
-            3,
-            [(v_banks[1], add_bias_scalar, nc.scalar, 0, middle), (v_banks[2], add_bias_vector, nc.sync, middle, ROW_TILES)],
-        )
-        second_layer(1, [(s_banks[1], add_bias_vector, nc.sync, 0, ROW_TILES)])
-        second_layer(2, [(v_banks[0], add_bias_scalar, nc.sync, 0, ROW_TILES)])
+        rows_last(3, last3)
+        second_layer(2, 1, [(h_banks[0], add_bias_scalar, nc.sync, 0, 4)])
+        quantize_h(3)
+        second_layer(3, 1, [(h_banks[1], add_bias_scalar, nc.scalar, 0, 2), (s_banks[0], add_bias_vector, nc.sync, 2, 4)])

@@ -51,11 +51,12 @@ def tile_list_pnet_bias_kernel(
         got_plane = tile("got_plane", [P, G * J], U8)
         got_codes = tile("got_codes", [P, G * J], U32)
 
-        make_identity(nc, ident[:])
         first_row = P - SCALE_ROWS
-        nc.vector.memset(tab_rows[0:first_row, :], 0)
-        nc.sync.dma_start(tab_rows[first_row:P, :], tab_scales[0].bitcast(I32))
-        nc.sync.dma_start(offsets[:], offs)
+
+        def load_list():
+            nc.vector.memset(tab_rows[0:first_row, :], 0)
+            nc.sync.dma_start(tab_rows[first_row:P, :], tab_scales[0].bitcast(I32))
+            nc.sync.dma_start(offsets[:], offs)
 
         def load_rows(name, src):
             raw = tile(name, [P, PACK, src.shape[1]], F32)
@@ -87,6 +88,8 @@ def tile_list_pnet_bias_kernel(
             with nc.allow_non_contiguous_dma(reason="one bias value a partition and row tile"):
                 nc.sync.dma_start(bias[:], b.rearrange("(q p) -> p q", p=P))
 
+        make_identity(nc, ident[:])
+        load_list()
         nc.vector.memset(w_plane[:], 0)
         load_words()
         load_w_plane()
@@ -242,12 +245,12 @@ def tile_list_pnet_bias_kernel(
                 add_bias(result, sums, lo, hi)
                 queue.dma_start(out_rows[:, lo:hi, cols], result[:])
 
-        w_dealt = tile("w_dealt", [P, PACK, P, 2], U8)
+        w_dealt = tile("w_dealt", [P, PACK, P], U16)
         w_plane_dealt = tile("w_plane_dealt", [P, PACK, P], U8)
 
         def deal_w():
-            nc.gpsimd.tensor_copy(w_dealt[:], w_codes[:].bitcast(U8).rearrange("p (m t e) -> p t m e", t=PACK, e=2))
-            nc.gpsimd.tensor_copy(w_plane_dealt[:], w_plane[:].bitcast(U8).rearrange("p (m t) -> p t m", t=PACK))
+            nc.vector.tensor_copy(w_dealt[:], w_codes[:].bitcast(U16).rearrange("p (m t) -> p t m", t=PACK))
+            nc.vector.tensor_copy(w_plane_dealt[:], w_plane[:].bitcast(U8).rearrange("p (m t) -> p t m", t=PACK))
 
         def round_wc(u):
             dst = wc_bf[:].rearrange("p (t m) i -> p m i t", t=PACK)[:, HALF // PACK * u : HALF // PACK * (u + 1), :, :]
@@ -275,7 +278,7 @@ def tile_list_pnet_bias_kernel(
                     cols = slice(J * g + CHUNK * k, J * g + CHUNK * (k + 1))
                     nc.tensor.matmul_mx(
                         out=dst,
-                        lhsT=w_dealt[:, t, :, :].rearrange("p m e -> p (m e)").bitcast(FP4X4),
+                        lhsT=w_dealt[:, t, :].bitcast(FP4X4),
                         lhsT_scale=w_plane_dealt[:, t, :],
                         rhs=got_codes[:, cols].bitcast(FP8X4),
                         rhs_scale=got_plane[:, cols],
@@ -322,41 +325,39 @@ def tile_list_pnet_bias_kernel(
         round_wc(1)
         pool_in(0, 1)
         pool_in(1, 1)
-        cast(on_scalar, c_bf, c_raw, 0, 2)
-        quantize_wc()
-        quantize_c(0, 2)
-        own_turned(0, s_banks[0])
-        own_turned(1, s_banks[1])
         rows_first(2, h_banks[0])
+        cast(on_scalar, c_bf, c_raw, 0, 2)
+        pool_in(0, 2)
+        quantize_wc()
+        pool_in(1, 2)
+        quantize_c(0, 2)
         rows_first(3, h_banks[1])
         cast(on_scalar, c_bf, c_raw, 2, 4)
-        pool_in(0, 2)
-        pool_in(1, 2)
         pool_in(0, 3)
         pool_in(1, 3)
-        quantize_c(2, 2)
+        own_turned(0, s_banks[0])
+        own_turned(1, s_banks[1])
+        cast(on_vector, wd_bf, wd_raw, 2, 4)
         rows_pool_in(2, 1)
+        quantize_c(2, 2)
+        cast(on_scalar, wd_bf, wd_raw, 0, 2)
         rows_pool_in(3, 1)
         rows_pool_in(2, 2)
-        rows_pool_in(3, 2)
-        own2 = rows_product(s_banks[0], 2, None, True)
         hidden(0, h_banks[0])
-        own3 = rows_product(s_banks[1], 3, None, True)
-        last2 = rows_product(v_banks[2], 2, 3, True)
+        own2 = rows_product(s_banks[0], 2, None, True)
+        own3 = rows_product(v_banks[2], 3, None, True)
         hidden(1, h_banks[1])
-        cast(on_scalar, wd_bf, wd_raw, 0, 2)
-        cast(on_vector, wd_bf, wd_raw, 2, 4)
+        last2 = rows_product(s_banks[1], 2, 3, True)
         quantize_wd()
-        quantize_h(0)
-        second_layer(0, 1, [(v_banks[0], add_bias_scalar, nc.sync, 0, 4)])
-        last3 = rows_product(v_banks[3], 3, 3, True)
         rows_add_own(2, own2)
-        quantize_h(1)
-        second_layer(1, 1, [(v_banks[1], add_bias_scalar, nc.sync, 0, 4)])
+        quantize_h(0, 2)
+        second_layer(0, 2, [(h_banks[0], add_bias_scalar, nc.sync, 0, 2), (h_banks[1], add_bias_scalar, nc.sync, 2, 4)])
+        rows_pool_in(3, 2)
         rows_last(2, last2)
+        last3 = rows_product(s_banks[0], 3, 3, True)
         rows_add_own(3, own3)
         quantize_h(2)
+        second_layer(2, 1, [(v_banks[3], add_bias_scalar, nc.sync, 0, 4)])
         rows_last(3, last3)
-        second_layer(2, 1, [(h_banks[0], add_bias_scalar, nc.sync, 0, 4)])
         quantize_h(3)
-        second_layer(3, 1, [(h_banks[1], add_bias_scalar, nc.scalar, 0, 2), (s_banks[0], add_bias_vector, nc.sync, 2, 4)])
+        second_layer(3, 1, [(v_banks[0], add_bias_scalar, nc.scalar, 0, 2), (v_banks[1], add_bias_vector, nc.sync, 2, 4)])

@@ -88,17 +88,18 @@ def tile_list_pnet_bias_kernel(
             with nc.allow_non_contiguous_dma(reason="one bias value a partition and row tile"):
                 nc.sync.dma_start(bias[:], b.rearrange("(q p) -> p q", p=P))
 
+        nc.gpsimd.memset(w_plane[:], 0)
         make_identity(nc, ident[:])
         load_list()
-        nc.vector.memset(w_plane[:], 0)
         load_words()
         load_w_plane()
         load_w_codes()
-        wc_raw = [load_rows("wc_raw0", wc[:, 0:HALF])]
+        wc_whole = load_rows("wc_raw", wc)
+        wc_raw = [wc_whole[:, :, 0:HALF], wc_whole[:, :, HALF:R]]
+        c_raw = [load_rows("c_raw0", c[:, 0:HALF])]
         gather_scales()
         move_scales(nc.sync)
-        wc_raw.append(load_rows("wc_raw1", wc[:, HALF:R]))
-        c_raw = load_rows("c_raw", c)
+        c_raw.append(load_rows("c_raw1", c[:, HALF:J]))
         wd_raw = load_rows("wd_raw", wd)
         load_bias()
 
@@ -120,7 +121,8 @@ def tile_list_pnet_bias_kernel(
         banks = [ps.tile([P, R], F32, name="bank%d" % i) for i in range(8)]
         s_banks, v_banks, h_banks = banks[0:2], banks[2:6], banks[6:8]
 
-        pooled = [tile("pooled%d" % k, [P, PACK, P], F32)[:] for k in range(CHUNKS)]
+        pooled = [tile("pooled%d" % k, [P, PACK, P], F32)[:] for k in range(2)]
+        pooled.extend(c_raw[1][:, 2 * i : 2 * i + 2, :].rearrange("p a (e m) -> p (a e) m", m=P) for i in range(2))
         own = [tile("own%d" % k, [P, PACK, P], F32) for k in range(CHUNKS)]
         wc_bf = tile("wc_bf", [P, R, PACK], BF16)
         c_bf = tile("c_bf", [P, J, PACK], BF16)
@@ -245,16 +247,20 @@ def tile_list_pnet_bias_kernel(
                 add_bias(result, sums, lo, hi)
                 queue.dma_start(out_rows[:, lo:hi, cols], result[:])
 
-        w_dealt = tile("w_dealt", [P, PACK, P], U16)
+        w_dealt = tile("w_dealt", [P, PACK, P, 2], U8)
         w_plane_dealt = tile("w_plane_dealt", [P, PACK, P], U8)
 
         def deal_w():
-            nc.vector.tensor_copy(w_dealt[:], w_codes[:].bitcast(U16).rearrange("p (m t) -> p t m", t=PACK))
-            nc.vector.tensor_copy(w_plane_dealt[:], w_plane[:].bitcast(U8).rearrange("p (m t) -> p t m", t=PACK))
+            nc.gpsimd.tensor_copy(w_dealt[:], w_codes[:].bitcast(U8).rearrange("p (m t e) -> p t m e", t=PACK, e=2))
+            nc.gpsimd.tensor_copy(w_plane_dealt[:], w_plane[:].bitcast(U8).rearrange("p (m t) -> p t m", t=PACK))
+
+        def round_wc_gpsimd(u):
+            dst = wc_bf[:].rearrange("p (t m) i -> p t m i", t=PACK)[:, :, HALF // PACK * u : HALF // PACK * (u + 1), :]
+            nc.gpsimd.tensor_scalar(dst, wc_raw[u].rearrange("p i (m t) -> p t m i", t=PACK), 1.0, 0.0, ALU.mult, ALU.add)
 
         def round_wc(u):
             dst = wc_bf[:].rearrange("p (t m) i -> p m i t", t=PACK)[:, HALF // PACK * u : HALF // PACK * (u + 1), :, :]
-            nc.scalar.copy(dst, wc_raw[u][:].rearrange("p i (m t) -> p m i t", t=PACK))
+            nc.scalar.copy(dst, wc_raw[u].rearrange("p i (m t) -> p m i t", t=PACK))
 
         def cast(on, dst, src, lo, hi):
             on(dst[:, P * lo : P * hi, :], src[:, :, P * lo : P * hi])
@@ -278,7 +284,7 @@ def tile_list_pnet_bias_kernel(
                     cols = slice(J * g + CHUNK * k, J * g + CHUNK * (k + 1))
                     nc.tensor.matmul_mx(
                         out=dst,
-                        lhsT=w_dealt[:, t, :].bitcast(FP4X4),
+                        lhsT=w_dealt[:, t, :, :].rearrange("p m e -> p (m e)").bitcast(FP4X4),
                         lhsT_scale=w_plane_dealt[:, t, :],
                         rhs=got_codes[:, cols].bitcast(FP8X4),
                         rhs_scale=got_plane[:, cols],
@@ -316,48 +322,102 @@ def tile_list_pnet_bias_kernel(
         def rows_last(k, sums):
             nc.vector.scalar_tensor_tensor(h_bf[:, points(k), :], sums, 0.0, woven(k), ALU.max, ALU.max)
 
+        wd_bf = c_bf
+
+        def product(step, bank):
+            kind, k, g = step
+            if kind == "points":
+                project(bank, g, k)
+                return dealt(bank)
+            return rows_product(bank, k, g, kind != "rows")
+
+        def fold(step, sums):
+            kind, k, g = step
+            if kind == "points":
+                nc.vector.tensor_tensor(pooled[k], sums, pooled[k], ALU.max)
+            elif kind == "rows":
+                nc.vector.tensor_tensor(woven(k), sums, woven(k), ALU.max)
+            elif kind == "own":
+                rows_add_own(k, sums)
+            else:
+                rows_last(k, sums)
+
+        waiting = []
+
+        def start_products(steps):
+            for step, bank in zip(steps, v_banks):
+                waiting.append((step, bank, product(step, bank)))
+            return steps[MAX_BANKS:]
+
+        def fold_next(then=None):
+            step, bank, sums = waiting.pop(0)
+            fold(step, sums)
+            if then is not None:
+                then()
+            if steps_left:
+                step = steps_left.pop(0)
+                waiting.append((step, bank, product(step, bank)))
+            return bank
+
+        def turn_in(bank, src, first):
+            for t in range(PACK):
+                nc.tensor.matmul(
+                    bank[:, CHUNK * t : CHUNK * (t + 1)],
+                    src[:, t, :],
+                    ident[:],
+                    is_transpose=True,
+                    start=(first and t == 0),
+                    stop=(not first and t == PACK - 1),
+                )
+
+        def finish_hidden(k, bank):
+            turn_in(bank, pooled[k], False)
+            nc.scalar.activation(h_bf[:, points(k), :], bank[:].rearrange("p (t j) -> p j t", t=PACK), ACT.Relu)
+
         gather_words(0, 2)
         gather_words(2, 2)
+        round_wc_gpsimd(1)
         deal_w()
         round_wc(0)
+        quantize_wc()
+        on_scalar(c_bf[:, 0:HALF, :], c_raw[0][:])
+        quantize_c(0, 2)
         first_neighbour(0, s_banks[0])
         first_neighbour(1, s_banks[1])
-        round_wc(1)
-        pool_in(0, 1)
-        pool_in(1, 1)
-        rows_first(2, h_banks[0])
-        cast(on_scalar, c_bf, c_raw, 0, 2)
-        pool_in(0, 2)
-        quantize_wc()
-        pool_in(1, 2)
-        quantize_c(0, 2)
-        rows_first(3, h_banks[1])
-        cast(on_scalar, c_bf, c_raw, 2, 4)
-        pool_in(0, 3)
-        pool_in(1, 3)
+        on_scalar(c_bf[:, HALF:J, :], c_raw[1][:])
+        quantize_c(2, 2)
+        cast(on_gpsimd, wd_bf, wd_raw, 2, 4)
+        steps_left = start_products(
+            [("points", 0, 1), ("points", 1, 1), ("points", 0, 2), ("points", 1, 2), ("points", 0, 3), ("points", 2, 1),
+             ("points", 1, 3), ("points", 2, 2), ("rows", 3, 1), ("points", 2, 3), ("rows", 3, 2), ("own", 3, None)]
+        )
         own_turned(0, s_banks[0])
         own_turned(1, s_banks[1])
-        cast(on_vector, wd_bf, wd_raw, 2, 4)
-        rows_pool_in(2, 1)
-        quantize_c(2, 2)
+        turn_in(s_banks[1], own[0], True)
+        first_neighbour(2, h_banks[0])
+        turn_in(h_banks[0], own[1], True)
+        rows_first(3, h_banks[1])
         cast(on_scalar, wd_bf, wd_raw, 0, 2)
-        rows_pool_in(3, 1)
-        rows_pool_in(2, 2)
-        hidden(0, h_banks[0])
-        own2 = rows_product(s_banks[0], 2, None, True)
-        own3 = rows_product(v_banks[2], 3, None, True)
-        hidden(1, h_banks[1])
-        last2 = rows_product(s_banks[1], 2, 3, True)
+        own_turned(2, s_banks[0])
+        turn_in(s_banks[0], own[2], True)
+        for i in range(4):
+            fold_next()
+        fold_next(lambda: finish_hidden(0, s_banks[1]))
+        fold_next()
+        fold_next(lambda: finish_hidden(1, h_banks[0]))
+        fold_next()
         quantize_wd()
-        rows_add_own(2, own2)
-        quantize_h(0, 2)
-        second_layer(0, 2, [(h_banks[0], add_bias_scalar, nc.sync, 0, 2), (h_banks[1], add_bias_scalar, nc.sync, 2, 4)])
-        rows_pool_in(3, 2)
-        rows_last(2, last2)
-        last3 = rows_product(s_banks[0], 3, 3, True)
-        rows_add_own(3, own3)
+        free0 = fold_next()
+        quantize_h(0)
+        second_layer(0, 1, [(h_banks[1], add_bias_scalar, nc.sync, 0, 4)])
+        free1 = fold_next(lambda: finish_hidden(2, s_banks[0]))
+        quantize_h(1)
+        second_layer(1, 1, [(s_banks[1], add_bias_scalar, nc.sync, 0, 4)])
+        last3 = rows_product(free0, 3, 3, True)
+        free2 = fold_next()
+        fold_next()
         quantize_h(2)
-        second_layer(2, 1, [(v_banks[3], add_bias_scalar, nc.sync, 0, 4)])
+        second_layer(2, 1, [(h_banks[0], add_bias_scalar, nc.sync, 0, 4)])
         rows_last(3, last3)
         quantize_h(3)
-        second_layer(3, 1, [(v_banks[0], add_bias_scalar, nc.scalar, 0, 2), (v_banks[1], add_bias_vector, nc.sync, 2, 4)])
+        second_layer(3, 1, [(free1, add_bias_scalar, nc.scalar, 0, 2), (free2, add_bias_vector, nc.sync, 2, 4)])

@@ -141,7 +141,7 @@ def tile_list_pnet_bias_kernel(
             return slice(CHUNK * k, CHUNK * (k + count))
 
         def dealt(bank):
-            return bank[:].rearrange("j (p t) -> j t p", t=PACK)
+            return bank[:].rearrange("j (t m) -> j t m", t=PACK)
 
         def gather_words(g, count):
             list_cols = slice(g * J // PER_COLUMN, (g + count) * J // PER_COLUMN)
@@ -154,8 +154,8 @@ def tile_list_pnet_bias_kernel(
                 out=bank[:],
                 lhsT=got_codes[:, cols].bitcast(FP8X4),
                 lhsT_scale=got_plane[:, cols],
-                rhs=w_codes[:].bitcast(U8).bitcast(FP4X4),
-                rhs_scale=w_plane[:].bitcast(U8),
+                rhs=w_dealt[:].rearrange("p t m e -> p (t m e)").bitcast(FP4X4),
+                rhs_scale=w_plane_dealt[:].rearrange("p t m -> p (t m)"),
                 start=True,
                 stop=True,
             )
@@ -406,15 +406,15 @@ def tile_list_pnet_bias_kernel(
         fold_next()
         fold_next(lambda: finish_hidden(1, h_banks[0]))
         fold_next()
-        quantize_wd()
         free0 = fold_next()
+        free1 = fold_next(lambda: finish_hidden(2, s_banks[0]))
+        quantize_wd()
         quantize_h(0)
         second_layer(0, 1, [(h_banks[1], add_bias_scalar, nc.sync, 0, 4)])
-        free1 = fold_next(lambda: finish_hidden(2, s_banks[0]))
-        quantize_h(1)
-        second_layer(1, 1, [(s_banks[1], add_bias_scalar, nc.sync, 0, 4)])
         last3 = rows_product(free0, 3, 3, True)
         free2 = fold_next()
+        quantize_h(1)
+        second_layer(1, 1, [(s_banks[1], add_bias_scalar, nc.sync, 0, 4)])
         fold_next()
         quantize_h(2)
         second_layer(2, 1, [(h_banks[0], add_bias_scalar, nc.sync, 0, 4)])

@@ -388,36 +388,33 @@ def tile_list_pnet_bias_kernel(
         quantize_c(2, 2)
         cast(on_gpsimd, wd_bf, wd_raw, 2, 4)
         steps_left = start_products(
-            [("points", 0, 1), ("points", 1, 1), ("points", 0, 2), ("points", 1, 2), ("points", 0, 3), ("points", 2, 1),
-             ("points", 1, 3), ("points", 2, 2), ("rows", 3, 1), ("points", 2, 3), ("rows", 3, 2), ("own", 3, None)]
+            [("points", 0, 1), ("points", 1, 1), ("points", 0, 2), ("points", 1, 2), ("points", 0, 3), ("rows", 2, 1),
+             ("points", 1, 3), ("rows", 3, 1), ("rows", 2, 2), ("rows", 3, 2), ("own", 2, None), ("last", 2, 3), ("own", 3, None)]
         )
         own_turned(0, s_banks[0])
         own_turned(1, s_banks[1])
         turn_in(s_banks[1], own[0], True)
-        first_neighbour(2, h_banks[0])
+        rows_first(2, h_banks[0])
         turn_in(h_banks[0], own[1], True)
         rows_first(3, h_banks[1])
         cast(on_scalar, wd_bf, wd_raw, 0, 2)
-        own_turned(2, s_banks[0])
-        turn_in(s_banks[0], own[2], True)
         for i in range(4):
             fold_next()
         fold_next(lambda: finish_hidden(0, s_banks[1]))
         fold_next()
         fold_next(lambda: finish_hidden(1, h_banks[0]))
         fold_next()
-        free0 = fold_next()
-        free1 = fold_next(lambda: finish_hidden(2, s_banks[0]))
+        fold_next()
         quantize_wd()
-        quantize_h(0)
-        second_layer(0, 1, [(h_banks[1], add_bias_scalar, nc.sync, 0, 4)])
-        last3 = rows_product(free0, 3, 3, True)
-        free2 = fold_next()
-        quantize_h(1)
-        second_layer(1, 1, [(s_banks[1], add_bias_scalar, nc.sync, 0, 4)])
+        free0 = fold_next()
+        quantize_h(0, 2)
+        second_layer(0, 2, [(h_banks[1], add_bias_scalar, nc.sync, 0, 2), (s_banks[1], add_bias_scalar, nc.sync, 2, 4)])
+        last3 = rows_product(s_banks[0], 3, 3, True)
+        free1 = fold_next()
+        fold_next()
         fold_next()
         quantize_h(2)
         second_layer(2, 1, [(h_banks[0], add_bias_scalar, nc.sync, 0, 4)])
         rows_last(3, last3)
         quantize_h(3)
-        second_layer(3, 1, [(free1, add_bias_scalar, nc.scalar, 0, 2), (free2, add_bias_vector, nc.sync, 2, 4)])
+        second_layer(3, 1, [(free0, add_bias_scalar, nc.scalar, 0, 2), (free1, add_bias_vector, nc.sync, 2, 4)])

@@ -94,8 +94,7 @@ def tile_list_pnet_bias_kernel(
         load_words()
         load_w_plane()
         load_w_codes()
-        wc_whole = load_rows("wc_raw", wc)
-        wc_raw = [wc_whole[:, :, 0:HALF], wc_whole[:, :, HALF:R]]
+        wc_raw = [load_rows("wc_raw%d" % u, wc[:, HALF * u : HALF * (u + 1)]) for u in range(2)]
         c_raw = [load_rows("c_raw0", c[:, 0:HALF])]
         gather_scales()
         move_scales(nc.sync)
@@ -256,11 +255,11 @@ def tile_list_pnet_bias_kernel(
 
         def round_wc_gpsimd(u):
             dst = wc_bf[:].rearrange("p (t m) i -> p t m i", t=PACK)[:, :, HALF // PACK * u : HALF // PACK * (u + 1), :]
-            nc.gpsimd.tensor_scalar(dst, wc_raw[u].rearrange("p i (m t) -> p t m i", t=PACK), 1.0, 0.0, ALU.mult, ALU.add)
+            nc.gpsimd.tensor_scalar(dst, wc_raw[u][:].rearrange("p i (m t) -> p t m i", t=PACK), 1.0, 0.0, ALU.mult, ALU.add)
 
         def round_wc(u):
             dst = wc_bf[:].rearrange("p (t m) i -> p m i t", t=PACK)[:, HALF // PACK * u : HALF // PACK * (u + 1), :, :]
-            nc.scalar.copy(dst, wc_raw[u].rearrange("p i (m t) -> p m i t", t=PACK))
+            nc.scalar.copy(dst, wc_raw[u][:].rearrange("p i (m t) -> p m i t", t=PACK))
 
         def cast(on, dst, src, lo, hi):
             on(dst[:, P * lo : P * hi, :], src[:, :, P * lo : P * hi])
@@ -376,9 +375,9 @@ def tile_list_pnet_bias_kernel(
 
         gather_words(0, 2)
         gather_words(2, 2)
-        round_wc_gpsimd(1)
         deal_w()
         round_wc(0)
+        round_wc(1)
         quantize_wc()
         on_scalar(c_bf[:, 0:HALF, :], c_raw[0][:])
         quantize_c(0, 2)

@@ -20,13 +20,14 @@ ACT = mybir.ActivationFunctionType
 P = 128
 PACK = 4
 QUADRANT = 32
+PLANE_ROWS = 4
 SCALE_ROWS = K // 32
 PER_COLUMN = 16
+LINE = 4
 CHUNK = 128
-CHUNKS = J // CHUNK
 HALF = 256
 ROW_TILES = N // P
-MAX_BANKS = 4
+LAST = G - 1
 
 
 def tile_list_pnet_bias_kernel(
@@ -51,13 +52,6 @@ def tile_list_pnet_bias_kernel(
         got_plane = tile("got_plane", [P, G * J], U8)
         got_codes = tile("got_codes", [P, G * J], U32)
 
-        first_row = P - SCALE_ROWS
-
-        def load_list():
-            nc.vector.memset(tab_rows[0:first_row, :], 0)
-            nc.sync.dma_start(tab_rows[first_row:P, :], tab_scales[0].bitcast(I32))
-            nc.sync.dma_start(offsets[:], offs)
-
         def load_rows(name, src):
             raw = tile(name, [P, PACK, src.shape[1]], F32)
             nc.sync.dma_start(raw[:], src.rearrange("(p i) x -> p i x", i=PACK))
@@ -66,66 +60,36 @@ def tile_list_pnet_bias_kernel(
         def plane_rows(r):
             return slice(r, P, QUADRANT)
 
-        def load_words():
-            nc.sync.dma_start(tab_codes[:], tab_words[0].rearrange("p t i -> p (t i)").bitcast(I32))
-
-        def load_w_plane():
-            for r in range(4):
-                nc.sync.dma_start(w_plane[plane_rows(r), :], w_scales[0, r:SCALE_ROWS:4, :].bitcast(I32))
-
-        def load_w_codes():
-            nc.sync.dma_start(w_codes[:], w_words[0].bitcast(I32))
-
-        def gather_scales():
-            nc.vector.tensor_copy(got_rows[:], tab_rows[:].bitcast(U8).indirect(offsets[:]))
-
-        def move_scales(queue):
-            for r in range(4):
-                rows = slice(first_row + r, P, 4)
-                queue.dma_start(got_plane[plane_rows(r), :].bitcast(I32), got_rows[rows, :].bitcast(I32))
-
-        def load_bias():
-            with nc.allow_non_contiguous_dma(reason="one bias value a partition and row tile"):
-                nc.sync.dma_start(bias[:], b.rearrange("(q p) -> p q", p=P))
-
         nc.gpsimd.memset(w_plane[:], 0)
         make_identity(nc, ident[:])
-        load_list()
-        load_words()
-        load_w_plane()
-        load_w_codes()
+        first_row = P - SCALE_ROWS
+        nc.vector.memset(tab_rows[0:first_row, :], 0)
+        nc.sync.dma_start(tab_rows[first_row:P, :], tab_scales[0].bitcast(I32))
+        nc.sync.dma_start(offsets[:], offs)
+        nc.sync.dma_start(tab_codes[:], tab_words[0].rearrange("p t i -> p (t i)").bitcast(I32))
+        for r in range(PLANE_ROWS):
+            nc.sync.dma_start(w_plane[plane_rows(r), :], w_scales[0, r:SCALE_ROWS:PLANE_ROWS, :].bitcast(I32))
+        nc.sync.dma_start(w_codes[:], w_words[0].bitcast(I32))
         wc_raw = [load_rows("wc_raw%d" % u, wc[:, HALF * u : HALF * (u + 1)]) for u in range(2)]
         c_raw = [load_rows("c_raw0", c[:, 0:HALF])]
-        gather_scales()
-        move_scales(nc.sync)
+        nc.vector.tensor_copy(got_rows[:], tab_rows[:].bitcast(U8).indirect(offsets[:]))
+        for r in range(PLANE_ROWS):
+            rows = slice(first_row + r, P, PLANE_ROWS)
+            nc.sync.dma_start(got_plane[plane_rows(r), :].bitcast(I32), got_rows[rows, :].bitcast(I32))
         c_raw.append(load_rows("c_raw1", c[:, HALF:J]))
         wd_raw = load_rows("wd_raw", wd)
-        load_bias()
-
-        def weave(copy, dst, src):
-            copy(dst.rearrange("p (x u) i -> p x i u", u=4), src.rearrange("p i (x u) -> p x i u", u=4))
-
-        def on_gpsimd(dst, src):
-            nc.gpsimd.tensor_scalar(dst, src.rearrange("p i x -> p x i"), 1.0, 0.0, ALU.mult, ALU.add)
-
-        def on_scalar(dst, src):
-            weave(nc.scalar.copy, dst, src)
-
-        def on_vector(dst, src):
-            weave(nc.vector.tensor_copy, dst, src)
-
-        def quantize(codes, plane, src):
-            nc.vector.quantize_mx(out=codes.bitcast(FP8X4), scales=plane, in_=src.rearrange("p x i -> p (x i)"))
+        with nc.allow_non_contiguous_dma(reason="one bias value a partition and row tile"):
+            nc.sync.dma_start(bias[:], b.rearrange("(q p) -> p q", p=P))
 
         banks = [ps.tile([P, R], F32, name="bank%d" % i) for i in range(8)]
-        s_banks, v_banks, h_banks = banks[0:2], banks[2:6], banks[6:8]
+        early_banks, fold_banks, late_banks = banks[0:2], banks[2:6], banks[6:8]
 
         pooled = [tile("pooled%d" % k, [P, PACK, P], F32)[:] for k in range(2)]
         pooled.extend(c_raw[1][:, 2 * i : 2 * i + 2, :].rearrange("p a (e m) -> p (a e) m", m=P) for i in range(2))
-        own = [tile("own%d" % k, [P, PACK, P], F32) for k in range(CHUNKS)]
+        own = [tile("own%d" % k, [P, PACK, P], F32) for k in range(2)]
         wc_bf = tile("wc_bf", [P, R, PACK], BF16)
         c_bf = tile("c_bf", [P, J, PACK], BF16)
-        wd_bf = tile("wd_bf", [P, N, PACK], BF16)
+        wd_bf = c_bf
         wc_codes = tile("wc_codes", [P, R], U32)
         wc_plane = tile("wc_plane", [P, R], U8)
         c_codes = tile("c_codes", [P, J], U32)
@@ -135,61 +99,61 @@ def tile_list_pnet_bias_kernel(
         h_bf = tile("h_bf", [P, J, PACK], BF16)
         h_codes = tile("h_codes", [P, J], U32)
         h_plane = tile("h_plane", [P, J], U8)
+        w_dealt = tile("w_dealt", [P, PACK, P, 2], U8)
+        w_plane_dealt = tile("w_plane_dealt", [P, PACK, P], U8)
+        top = {k: tile("top%d" % k, [P, CHUNK, PACK], BF16) for k in (2, 3)}
 
         def points(k, count=1):
             return slice(CHUNK * k, CHUNK * (k + count))
 
-        def dealt(bank):
-            return bank[:].rearrange("j (t m) -> j t m", t=PACK)
+        def entries(g, k):
+            return slice(J * g + CHUNK * k, J * g + CHUNK * (k + 1))
 
         def gather_words(g, count):
             list_cols = slice(g * J // PER_COLUMN, (g + count) * J // PER_COLUMN)
             picked = tab_codes[:].bitcast(U32).indirect(offsets[:, list_cols])
             nc.vector.tensor_copy(got_codes[:, g * J : (g + count) * J], picked)
 
-        def project(bank, g, k):
-            cols = slice(J * g + CHUNK * k, J * g + CHUNK * (k + 1))
+        def deal_w():
+            nc.gpsimd.tensor_copy(w_dealt[:], w_codes[:].bitcast(U8).rearrange("p (m t e) -> p t m e", t=PACK, e=2))
+            nc.gpsimd.tensor_copy(w_plane_dealt[:], w_plane[:].bitcast(U8).rearrange("p (m t) -> p t m", t=PACK))
+
+        def round_wc(u):
+            places = slice(HALF // PACK * u, HALF // PACK * (u + 1))
+            dst = wc_bf[:].rearrange("p (t m) i -> p m i t", t=PACK)[:, places, :, :]
+            nc.scalar.copy(dst, wc_raw[u][:].rearrange("p i (m t) -> p m i t", t=PACK))
+
+        def round_on_scalar(dst, src):
+            nc.scalar.copy(
+                dst.rearrange("p (x u) i -> p x i u", u=LINE), src.rearrange("p i (x u) -> p x i u", u=LINE)
+            )
+
+        def round_on_gpsimd(dst, src):
+            nc.gpsimd.tensor_scalar(dst, src.rearrange("p i x -> p x i"), 1.0, 0.0, ALU.mult, ALU.add)
+
+        def quantize(codes, plane, src):
+            nc.vector.quantize_mx(out=codes.bitcast(FP8X4), scales=plane, in_=src.rearrange("p x i -> p (x i)"))
+
+        def quantize_columns(codes, plane, src, k, count=1):
+            cols = points(k, count)
+            quantize(codes[:, cols], plane[:, cols], src[:, cols, :])
+
+        def by_points(bank):
+            return bank[:].rearrange("j (t m) -> j t m", t=PACK)
+
+        def neighbour_by_points(bank, k, g):
             nc.tensor.matmul_mx(
                 out=bank[:],
-                lhsT=got_codes[:, cols].bitcast(FP8X4),
-                lhsT_scale=got_plane[:, cols],
+                lhsT=got_codes[:, entries(g, k)].bitcast(FP8X4),
+                lhsT_scale=got_plane[:, entries(g, k)],
                 rhs=w_dealt[:].rearrange("p t m e -> p (t m e)").bitcast(FP4X4),
                 rhs_scale=w_plane_dealt[:].rearrange("p t m -> p (t m)"),
                 start=True,
                 stop=True,
             )
+            return by_points(bank)
 
-        def to_sbuf(dst, k, g, bank):
-            project(bank, g, k)
-            nc.scalar.copy(dst, dealt(bank))
-
-        def first_neighbour(k, bank):
-            to_sbuf(pooled[k], k, 0, bank)
-
-        maxima_done = []
-
-        def pool_in(k, g, dst=None):
-            dst = pooled[k] if dst is None else dst
-            bank = v_banks[len(maxima_done) % MAX_BANKS]
-            maxima_done.append((k, g))
-            project(bank, g, k)
-            nc.vector.tensor_tensor(dst, dealt(bank), dst, ALU.max)
-
-        def quantize_wc():
-            quantize(wc_codes[:], wc_plane[:], wc_bf[:])
-
-        def quantize_wd():
-            quantize(wd_codes[:], wd_plane[:], wd_bf[:])
-
-        def quantize_c(k, count):
-            cols = points(k, count)
-            quantize(c_codes[:, cols], c_plane[:, cols], c_bf[:, cols, :])
-
-        def quantize_h(k, count=1):
-            cols = points(k, count)
-            quantize(h_codes[:, cols], h_plane[:, cols], h_bf[:, cols, :])
-
-        def own_projection(k, bank):
+        def own_by_points(bank, k):
             nc.tensor.matmul_mx(
                 out=bank[:],
                 lhsT=c_codes[:, points(k)].bitcast(FP8X4),
@@ -199,34 +163,103 @@ def tile_list_pnet_bias_kernel(
                 start=True,
                 stop=True,
             )
-            nc.scalar.copy(own[k][:], dealt(bank))
+            nc.scalar.copy(own[k][:], by_points(bank))
 
-        def turn(bank, first, second):
-            for s, src in enumerate((first, second)):
-                for t in range(PACK):
-                    nc.tensor.matmul(
-                        bank[:, CHUNK * t : CHUNK * (t + 1)],
-                        src[:, t, :],
-                        ident[:],
-                        is_transpose=True,
-                        start=(s == 0 and t == 0),
-                        stop=(s == 1 and t == PACK - 1),
-                    )
+        def woven_view(bank):
             return bank[:].rearrange("p (t j) -> p j t", t=PACK)
 
-        def hidden(k, bank):
-            nc.scalar.activation(h_bf[:, points(k), :], turn(bank, own[k], pooled[k]), ACT.Relu)
+        def transpose_into(bank, src, opens):
+            for t in range(PACK):
+                nc.tensor.matmul(
+                    bank[:, CHUNK * t : CHUNK * (t + 1)],
+                    src[:, t, :],
+                    ident[:],
+                    is_transpose=True,
+                    start=(opens and t == 0),
+                    stop=(not opens and t == PACK - 1),
+                )
+
+        def finish_by_points(bank, k):
+            transpose_into(bank, pooled[k], False)
+            nc.scalar.activation(h_bf[:, points(k), :], woven_view(bank), ACT.Relu)
+
+        def product_by_rows(bank, k, g, with_own):
+            for t in range(PACK):
+                dst = bank[:, CHUNK * t : CHUNK * (t + 1)]
+                if g is not None:
+                    nc.tensor.matmul_mx(
+                        out=dst,
+                        lhsT=w_dealt[:, t, :, :].rearrange("p m e -> p (m e)").bitcast(FP4X4),
+                        lhsT_scale=w_plane_dealt[:, t, :],
+                        rhs=got_codes[:, entries(g, k)].bitcast(FP8X4),
+                        rhs_scale=got_plane[:, entries(g, k)],
+                        start=True,
+                        stop=not with_own,
+                    )
+                if with_own:
+                    nc.tensor.matmul_mx(
+                        out=dst,
+                        lhsT=wc_codes[:, P * t : P * (t + 1)].bitcast(FP8X4),
+                        lhsT_scale=wc_plane[:, P * t : P * (t + 1)],
+                        rhs=c_codes[:, points(k)].bitcast(FP8X4),
+                        rhs_scale=c_plane[:, points(k)],
+                        start=g is None,
+                        stop=True,
+                    )
+            return woven_view(bank)
+
+        def pooled_woven(k):
+            return pooled[k].rearrange("p a b -> p (a b)").rearrange("p (j t) -> p j t", t=PACK)
+
+        def top_candidate(bank, k):
+            nc.scalar.activation(top[k][:], product_by_rows(bank, k, LAST, True), ACT.Relu)
+
+        def larger_candidate(k):
+            flat = h_bf[:, points(k), :].rearrange("p j t -> p (j t)")
+            nc.vector.tensor_tensor(flat, flat, top[k][:].rearrange("p j t -> p (j t)"), ALU.max)
+
+        def product(step, bank):
+            k, g = step
+            if k < 2:
+                return neighbour_by_points(bank, k, g)
+            return product_by_rows(bank, k, g, g is None)
+
+        def fold(step, sums):
+            k, g = step
+            if k < 2:
+                nc.vector.tensor_tensor(pooled[k], sums, pooled[k], ALU.max)
+            elif g is not None:
+                nc.vector.tensor_tensor(pooled_woven(k), sums, pooled_woven(k), ALU.max)
+            else:
+                nc.vector.tensor_tensor(h_bf[:, points(k), :], sums, pooled_woven(k), ALU.add)
+
+        steps = [(0, 1), (1, 1), (0, 2), (1, 2), (0, 3), (2, 1), (1, 3), (3, 1), (2, 2), (3, 2), (2, None), (3, None)]
+        waiting = []
+
+        def start_product(bank):
+            step = steps.pop(0)
+            waiting.append((step, bank, product(step, bank)))
+
+        def fold_next(finish_in=None):
+            step, bank, sums = waiting.pop(0)
+            fold(step, sums)
+            if finish_in is not None:
+                finish_by_points(finish_in, step[0])
+            if steps:
+                start_product(bank)
+            return bank
 
         out_rows = out.rearrange("(q p) j -> p q j", p=P)
 
-        def add_bias_scalar(dst, sums, lo, hi):
+        def bias_on_scalar(dst, sums, lo, hi):
             for q in range(lo, hi):
                 nc.scalar.activation(dst[:, q - lo, :], sums[:, q - lo, :], ACT.Identity, bias=bias[:, q : q + 1])
 
-        def add_bias_vector(dst, sums, lo, hi):
+        def bias_on_vector(dst, sums, lo, hi):
             nc.vector.tensor_tensor(dst[:], sums, bias[:, lo:hi].unsqueeze(2).to_broadcast(list(sums.shape)), ALU.add)
 
         def second_layer(k, count, shares):
+            quantize_columns(h_codes, h_plane, h_bf, k, count)
             width = CHUNK * count
             cols = points(k, count)
             for bank, add_bias, queue, lo, hi in shares:
@@ -246,174 +279,45 @@ def tile_list_pnet_bias_kernel(
                 add_bias(result, sums, lo, hi)
                 queue.dma_start(out_rows[:, lo:hi, cols], result[:])
 
-        w_dealt = tile("w_dealt", [P, PACK, P, 2], U8)
-        w_plane_dealt = tile("w_plane_dealt", [P, PACK, P], U8)
-
-        def deal_w():
-            nc.gpsimd.tensor_copy(w_dealt[:], w_codes[:].bitcast(U8).rearrange("p (m t e) -> p t m e", t=PACK, e=2))
-            nc.gpsimd.tensor_copy(w_plane_dealt[:], w_plane[:].bitcast(U8).rearrange("p (m t) -> p t m", t=PACK))
-
-        def round_wc_gpsimd(u):
-            dst = wc_bf[:].rearrange("p (t m) i -> p t m i", t=PACK)[:, :, HALF // PACK * u : HALF // PACK * (u + 1), :]
-            nc.gpsimd.tensor_scalar(dst, wc_raw[u][:].rearrange("p i (m t) -> p t m i", t=PACK), 1.0, 0.0, ALU.mult, ALU.add)
-
-        def round_wc(u):
-            dst = wc_bf[:].rearrange("p (t m) i -> p m i t", t=PACK)[:, HALF // PACK * u : HALF // PACK * (u + 1), :, :]
-            nc.scalar.copy(dst, wc_raw[u][:].rearrange("p i (m t) -> p m i t", t=PACK))
-
-        def cast(on, dst, src, lo, hi):
-            on(dst[:, P * lo : P * hi, :], src[:, :, P * lo : P * hi])
-
-        def own_turned(k, bank):
-            nc.tensor.matmul_mx(
-                out=bank[:],
-                lhsT=c_codes[:, points(k)].bitcast(FP8X4),
-                lhsT_scale=c_plane[:, points(k)],
-                rhs=wc_codes[:].bitcast(FP8X4),
-                rhs_scale=wc_plane[:],
-                start=True,
-                stop=True,
-            )
-            nc.scalar.copy(own[k][:], bank[:].rearrange("j (t m) -> j t m", t=PACK))
-
-        def rows_product(bank, k, g, with_own):
-            for t in range(PACK):
-                dst = bank[:, CHUNK * t : CHUNK * (t + 1)]
-                if g is not None:
-                    cols = slice(J * g + CHUNK * k, J * g + CHUNK * (k + 1))
-                    nc.tensor.matmul_mx(
-                        out=dst,
-                        lhsT=w_dealt[:, t, :, :].rearrange("p m e -> p (m e)").bitcast(FP4X4),
-                        lhsT_scale=w_plane_dealt[:, t, :],
-                        rhs=got_codes[:, cols].bitcast(FP8X4),
-                        rhs_scale=got_plane[:, cols],
-                        start=True,
-                        stop=not with_own,
-                    )
-                if with_own:
-                    nc.tensor.matmul_mx(
-                        out=dst,
-                        lhsT=wc_codes[:, P * t : P * (t + 1)].bitcast(FP8X4),
-                        lhsT_scale=wc_plane[:, P * t : P * (t + 1)],
-                        rhs=c_codes[:, points(k)].bitcast(FP8X4),
-                        rhs_scale=c_plane[:, points(k)],
-                        start=g is None,
-                        stop=True,
-                    )
-            return bank[:].rearrange("p (t j) -> p j t", t=PACK)
-
-        def woven(k):
-            return pooled[k].rearrange("p a b -> p (a b)").rearrange("p (j t) -> p j t", t=PACK)
-
-        def take_bank():
-            maxima_done.append(None)
-            return v_banks[(len(maxima_done) - 1) % MAX_BANKS]
-
-        def rows_first(k, bank):
-            nc.scalar.copy(woven(k), rows_product(bank, k, 0, False))
-
-        def rows_pool_in(k, g):
-            nc.vector.tensor_tensor(woven(k), rows_product(take_bank(), k, g, False), woven(k), ALU.max)
-
-        def rows_add_own(k, sums):
-            nc.vector.tensor_tensor(woven(k), sums, woven(k), ALU.add)
-
-        def rows_last(k, sums):
-            nc.vector.scalar_tensor_tensor(h_bf[:, points(k), :], sums, 0.0, woven(k), ALU.max, ALU.max)
-
-        wd_bf = c_bf
-
-        def product(step, bank):
-            kind, k, g = step
-            if kind == "points":
-                project(bank, g, k)
-                return dealt(bank)
-            return rows_product(bank, k, g, kind != "rows")
-
-        def fold(step, sums):
-            kind, k, g = step
-            if kind == "points":
-                nc.vector.tensor_tensor(pooled[k], sums, pooled[k], ALU.max)
-            elif kind == "rows":
-                nc.vector.tensor_tensor(woven(k), sums, woven(k), ALU.max)
-            elif kind == "own":
-                rows_add_own(k, sums)
-            else:
-                rows_last(k, sums)
-
-        waiting = []
-
-        def start_products(steps):
-            for step, bank in zip(steps, v_banks):
-                waiting.append((step, bank, product(step, bank)))
-            return steps[MAX_BANKS:]
-
-        def fold_next(then=None):
-            step, bank, sums = waiting.pop(0)
-            fold(step, sums)
-            if then is not None:
-                then()
-            if steps_left:
-                step = steps_left.pop(0)
-                waiting.append((step, bank, product(step, bank)))
-            return bank
-
-        def turn_in(bank, src, first):
-            for t in range(PACK):
-                nc.tensor.matmul(
-                    bank[:, CHUNK * t : CHUNK * (t + 1)],
-                    src[:, t, :],
-                    ident[:],
-                    is_transpose=True,
-                    start=(first and t == 0),
-                    stop=(not first and t == PACK - 1),
-                )
-
-        def finish_hidden(k, bank):
-            turn_in(bank, pooled[k], False)
-            nc.scalar.activation(h_bf[:, points(k), :], bank[:].rearrange("p (t j) -> p j t", t=PACK), ACT.Relu)
-
         gather_words(0, 2)
         gather_words(2, 2)
         deal_w()
         round_wc(0)
         round_wc(1)
-        quantize_wc()
-        on_scalar(c_bf[:, 0:HALF, :], c_raw[0][:])
-        quantize_c(0, 2)
-        first_neighbour(0, s_banks[0])
-        first_neighbour(1, s_banks[1])
-        on_scalar(c_bf[:, HALF:J, :], c_raw[1][:])
-        quantize_c(2, 2)
-        cast(on_gpsimd, wd_bf, wd_raw, 2, 4)
-        steps_left = start_products(
-            [("points", 0, 1), ("points", 1, 1), ("points", 0, 2), ("points", 1, 2), ("points", 0, 3), ("rows", 2, 1),
-             ("points", 1, 3), ("rows", 3, 1), ("rows", 2, 2), ("rows", 3, 2), ("own", 2, None), ("last", 2, 3), ("own", 3, None)]
-        )
-        own_turned(0, s_banks[0])
-        own_turned(1, s_banks[1])
-        turn_in(s_banks[1], own[0], True)
-        rows_first(2, h_banks[0])
-        turn_in(h_banks[0], own[1], True)
-        rows_first(3, h_banks[1])
-        cast(on_scalar, wd_bf, wd_raw, 0, 2)
-        for i in range(4):
+        quantize(wc_codes[:], wc_plane[:], wc_bf[:])
+        round_on_scalar(c_bf[:, 0:HALF, :], c_raw[0][:])
+        quantize_columns(c_codes, c_plane, c_bf, 0, 2)
+        for k in range(2):
+            nc.scalar.copy(pooled[k], neighbour_by_points(early_banks[k], k, 0))
+        round_on_scalar(c_bf[:, HALF:J, :], c_raw[1][:])
+        quantize_columns(c_codes, c_plane, c_bf, 2, 2)
+        round_on_gpsimd(wd_bf[:, HALF:N, :], wd_raw[:, :, HALF:N])
+        for bank in fold_banks:
+            start_product(bank)
+
+        own_by_points(early_banks[0], 0)
+        own_by_points(early_banks[1], 1)
+        transpose_into(early_banks[1], own[0], True)
+        nc.scalar.copy(pooled_woven(2), product_by_rows(late_banks[0], 2, 0, False))
+        transpose_into(late_banks[0], own[1], True)
+        nc.scalar.copy(pooled_woven(3), product_by_rows(late_banks[1], 3, 0, False))
+        round_on_scalar(wd_bf[:, 0:HALF, :], wd_raw[:, :, 0:HALF])
+
+        for _ in range(4):
             fold_next()
-        fold_next(lambda: finish_hidden(0, s_banks[1]))
+        fold_next(finish_in=early_banks[1])
         fold_next()
-        fold_next(lambda: finish_hidden(1, h_banks[0]))
+        fold_next(finish_in=late_banks[0])
+        top_candidate(early_banks[0], 2)
+        fold_next()
+        free_first = fold_next()
+        top_candidate(late_banks[1], 3)
+        quantize(wd_codes[:], wd_plane[:], wd_bf[:])
+        free_second = fold_next()
+        second_layer(0, 2, [(free_first, bias_on_scalar, nc.sync, 0, 2), (early_banks[1], bias_on_scalar, nc.sync, 2, 4)])
         fold_next()
         fold_next()
-        quantize_wd()
-        free0 = fold_next()
-        quantize_h(0, 2)
-        second_layer(0, 2, [(h_banks[1], add_bias_scalar, nc.sync, 0, 2), (s_banks[1], add_bias_scalar, nc.sync, 2, 4)])
-        last3 = rows_product(s_banks[0], 3, 3, True)
-        free1 = fold_next()
-        fold_next()
-        fold_next()
-        quantize_h(2)
-        second_layer(2, 1, [(h_banks[0], add_bias_scalar, nc.sync, 0, 4)])
-        rows_last(3, last3)
-        quantize_h(3)
-        second_layer(3, 1, [(free0, add_bias_scalar, nc.scalar, 0, 2), (free1, add_bias_vector, nc.sync, 2, 4)])
+        larger_candidate(2)
+        second_layer(2, 1, [(late_banks[0], bias_on_scalar, nc.sync, 0, 4)])
+        larger_candidate(3)
+        second_layer(3, 1, [(free_second, bias_on_scalar, nc.scalar, 0, 2), (early_banks[0], bias_on_vector, nc.sync, 2, 4)])

@@ -318,6 +318,6 @@ def tile_list_pnet_bias_kernel(
         fold_next()
         fold_next()
         larger_candidate(2)
-        second_layer(2, 1, [(late_banks[0], bias_on_scalar, nc.sync, 0, 4)])
+        second_layer(2, 1, [(late_banks[0], bias_on_scalar, nc.sync, 0, 2), (late_banks[1], bias_on_scalar, nc.sync, 2, 4)])
         larger_candidate(3)
-        second_layer(3, 1, [(free_second, bias_on_scalar, nc.scalar, 0, 2), (early_banks[0], bias_on_vector, nc.sync, 2, 4)])
+        second_layer(3, 1, [(early_banks[0], bias_on_vector, nc.sync, 2, 4), (free_second, bias_on_scalar, nc.scalar, 0, 2)])

@@ -36,6 +36,7 @@ def tile_list_pnet_bias_kernel(
     nc = tc.nc
     with ExitStack() as ctx:
         sb = ctx.enter_context(tc.tile_pool(name="sb", bufs=1))
+        shared = ctx.enter_context(tc.tile_pool(name="shared", bufs=1))
         ps = ctx.enter_context(tc.psum_pool(name="ps", bufs=1))
 
         def tile(name, shape, dtype):
@@ -70,13 +71,12 @@ def tile_list_pnet_bias_kernel(
         for r in range(PLANE_ROWS):
             nc.sync.dma_start(w_plane[plane_rows(r), :], w_scales[0, r:SCALE_ROWS:PLANE_ROWS, :].bitcast(I32))
         nc.sync.dma_start(w_codes[:], w_words[0].bitcast(I32))
-        wc_raw = [load_rows("wc_raw%d" % u, wc[:, HALF * u : HALF * (u + 1)]) for u in range(2)]
-        c_raw = [load_rows("c_raw0", c[:, 0:HALF])]
+        wc_raw = load_rows("wc_raw", wc)
         nc.vector.tensor_copy(got_rows[:], tab_rows[:].bitcast(U8).indirect(offsets[:]))
         for r in range(PLANE_ROWS):
             rows = slice(first_row + r, P, PLANE_ROWS)
             nc.sync.dma_start(got_plane[plane_rows(r), :].bitcast(I32), got_rows[rows, :].bitcast(I32))
-        c_raw.append(load_rows("c_raw1", c[:, HALF:J]))
+        c_raw = load_rows("c_raw", c)
         wd_raw = load_rows("wd_raw", wd)
         with nc.allow_non_contiguous_dma(reason="one bias value a partition and row tile"):
             nc.sync.dma_start(bias[:], b.rearrange("(q p) -> p q", p=P))
@@ -84,12 +84,17 @@ def tile_list_pnet_bias_kernel(
         banks = [ps.tile([P, R], F32, name="bank%d" % i) for i in range(8)]
         early_banks, fold_banks, late_banks = banks[0:2], banks[2:6], banks[6:8]
 
-        pooled = [tile("pooled%d" % k, [P, PACK, P], F32)[:] for k in range(2)]
-        pooled.extend(c_raw[1][:, 2 * i : 2 * i + 2, :].rearrange("p a (e m) -> p (a e) m", m=P) for i in range(2))
+        def placed(name, shape, dtype, offset):
+            return shared.tile(shape, dtype, name=name, align_bytes=64, offset=offset)
+
+        wc_bf = placed("wc_bf", [P, R, PACK], BF16, 0)
+        c_bf = [placed("c_bf0", [P, HALF, PACK], BF16, 6144), placed("c_bf1", [P, HALF, PACK], BF16, 2048)]
+        wd_bf = placed("wd_bf", [P, N, PACK], BF16, 3072)
+        second = placed("second", [P, 2, PACK, P], F32, 7168)
+        first = [tile("first%d" % k, [P, PACK, P], F32)[:] for k in range(2)]
+        pooled = [second[:, 0], second[:, 1]]
+        pooled.extend(c_raw[:, i, :].rearrange("p (e m) -> p e m", m=P) for i in range(2))
         own = [tile("own%d" % k, [P, PACK, P], F32) for k in range(2)]
-        wc_bf = tile("wc_bf", [P, R, PACK], BF16)
-        c_bf = tile("c_bf", [P, J, PACK], BF16)
-        wd_bf = c_bf
         wc_codes = tile("wc_codes", [P, R], U32)
         wc_plane = tile("wc_plane", [P, R], U8)
         c_codes = tile("c_codes", [P, J], U32)
@@ -118,10 +123,9 @@ def tile_list_pnet_bias_kernel(
             nc.gpsimd.tensor_copy(w_dealt[:], w_codes[:].bitcast(U8).rearrange("p (m t e) -> p t m e", t=PACK, e=2))
             nc.gpsimd.tensor_copy(w_plane_dealt[:], w_plane[:].bitcast(U8).rearrange("p (m t) -> p t m", t=PACK))
 
-        def round_wc(u):
-            places = slice(HALF // PACK * u, HALF // PACK * (u + 1))
-            dst = wc_bf[:].rearrange("p (t m) i -> p m i t", t=PACK)[:, places, :, :]
-            nc.scalar.copy(dst, wc_raw[u][:].rearrange("p i (m t) -> p m i t", t=PACK))
+        def round_wc():
+            dst = wc_bf[:].rearrange("p (t m) i -> p m i t", t=PACK)
+            nc.scalar.copy(dst, wc_raw[:].rearrange("p i (m t) -> p m i t", t=PACK))
 
         def round_on_scalar(dst, src):
             nc.scalar.copy(
@@ -227,7 +231,9 @@ def tile_list_pnet_bias_kernel(
         def fold(step, sums):
             k, g = step
             if k < 2:
-                nc.vector.tensor_tensor(pooled[k], sums, pooled[k], ALU.max)
+                moves_at = LAST - k
+                so_far = first[k] if g <= moves_at else pooled[k]
+                nc.vector.tensor_tensor(first[k] if g < moves_at else pooled[k], sums, so_far, ALU.max)
             elif g is not None:
                 nc.vector.tensor_tensor(pooled_woven(k), sums, pooled_woven(k), ALU.max)
             else:
@@ -282,16 +288,15 @@ def tile_list_pnet_bias_kernel(
         gather_words(0, 2)
         gather_words(2, 2)
         deal_w()
-        round_wc(0)
-        round_wc(1)
+        round_wc()
         quantize(wc_codes[:], wc_plane[:], wc_bf[:])
-        round_on_scalar(c_bf[:, 0:HALF, :], c_raw[0][:])
-        quantize_columns(c_codes, c_plane, c_bf, 0, 2)
         for k in range(2):
-            nc.scalar.copy(pooled[k], neighbour_by_points(early_banks[k], k, 0))
-        round_on_scalar(c_bf[:, HALF:J, :], c_raw[1][:])
-        quantize_columns(c_codes, c_plane, c_bf, 2, 2)
-        round_on_gpsimd(wd_bf[:, HALF:N, :], wd_raw[:, :, HALF:N])
+            nc.scalar.copy(first[k], neighbour_by_points(early_banks[k], k, 0))
+        round_on_gpsimd(c_bf[1][:], c_raw[:, :, HALF:J])
+        round_on_scalar(c_bf[0][:], c_raw[:, :, 0:HALF])
+        for u in (1, 0):
+            quantize(c_codes[:, HALF * u : HALF * (u + 1)], c_plane[:, HALF * u : HALF * (u + 1)], c_bf[u][:])
+        round_on_gpsimd(wd_bf[:], wd_raw[:])
         for bank in fold_banks:
             start_product(bank)
 
@@ -301,7 +306,6 @@ def tile_list_pnet_bias_kernel(
         nc.scalar.copy(pooled_woven(2), product_by_rows(late_banks[0], 2, 0, False))
         transpose_into(late_banks[0], own[1], True)
         nc.scalar.copy(pooled_woven(3), product_by_rows(late_banks[1], 3, 0, False))
-        round_on_scalar(wd_bf[:, 0:HALF, :], wd_raw[:, :, 0:HALF])
 
         for _ in range(4):
             fold_next()

@@ -27,6 +27,7 @@ LINE = 4
 CHUNK = 128
 HALF = 256
 ROW_TILES = N // P
+C_ON_SCALAR = 320
 LAST = G - 1
 
 
@@ -53,9 +54,9 @@ def tile_list_pnet_bias_kernel(
         got_plane = tile("got_plane", [P, G * J], U8)
         got_codes = tile("got_codes", [P, G * J], U32)
 
-        def load_rows(name, src):
-            raw = tile(name, [P, PACK, src.shape[1]], F32)
-            nc.sync.dma_start(raw[:], src.rearrange("(p i) x -> p i x", i=PACK))
+        def load_rows(name, src, lo, hi):
+            raw = tile(name, [P, PACK, hi - lo], F32)
+            nc.sync.dma_start(raw[:], src.rearrange("(p i) x -> p i x", i=PACK)[:, :, lo:hi])
             return raw
 
         def plane_rows(r):
@@ -71,13 +72,13 @@ def tile_list_pnet_bias_kernel(
         for r in range(PLANE_ROWS):
             nc.sync.dma_start(w_plane[plane_rows(r), :], w_scales[0, r:SCALE_ROWS:PLANE_ROWS, :].bitcast(I32))
         nc.sync.dma_start(w_codes[:], w_words[0].bitcast(I32))
-        wc_raw = load_rows("wc_raw", wc)
+        wc_raw = [load_rows("wc_raw%d" % u, wc, HALF * u, HALF * (u + 1)) for u in range(2)]
         nc.vector.tensor_copy(got_rows[:], tab_rows[:].bitcast(U8).indirect(offsets[:]))
         for r in range(PLANE_ROWS):
             rows = slice(first_row + r, P, PLANE_ROWS)
             nc.sync.dma_start(got_plane[plane_rows(r), :].bitcast(I32), got_rows[rows, :].bitcast(I32))
-        c_raw = load_rows("c_raw", c)
-        wd_raw = load_rows("wd_raw", wd)
+        c_raw = load_rows("c_raw", c, 0, J)
+        wd_raw = load_rows("wd_raw", wd, 0, N)
         with nc.allow_non_contiguous_dma(reason="one bias value a partition and row tile"):
             nc.sync.dma_start(bias[:], b.rearrange("(q p) -> p q", p=P))
 
@@ -88,10 +89,11 @@ def tile_list_pnet_bias_kernel(
             return shared.tile(shape, dtype, name=name, align_bytes=64, offset=offset)
 
         wc_bf = placed("wc_bf", [P, R, PACK], BF16, 0)
-        c_bf = [placed("c_bf0", [P, HALF, PACK], BF16, 6144), placed("c_bf1", [P, HALF, PACK], BF16, 2048)]
-        wd_bf = placed("wd_bf", [P, N, PACK], BF16, 3072)
-        second = placed("second", [P, 2, PACK, P], F32, 7168)
-        first = [tile("first%d" % k, [P, PACK, P], F32)[:] for k in range(2)]
+        c_bf = placed("c_bf", [P, J, PACK], BF16, 2048)
+        wd_bf = placed("wd_bf", [P, N, PACK], BF16, 0)
+        second = placed("second", [P, 2, PACK, P], F32, 4096)
+        spent = wc_raw[1][:].rearrange("p (k a) (b m) -> p k (a b) m", k=2, m=P)
+        first = [spent[:, 0], spent[:, 1]]
         pooled = [second[:, 0], second[:, 1]]
         pooled.extend(c_raw[:, i, :].rearrange("p (e m) -> p e m", m=P) for i in range(2))
         own = [tile("own%d" % k, [P, PACK, P], F32) for k in range(2)]
@@ -101,12 +103,16 @@ def tile_list_pnet_bias_kernel(
         c_plane = tile("c_plane", [P, J], U8)
         wd_codes = tile("wd_codes", [P, N], U32)
         wd_plane = tile("wd_plane", [P, N], U8)
-        h_bf = tile("h_bf", [P, J, PACK], BF16)
+        h_bf = tile("h_bf", [P, J - CHUNK, PACK], BF16)
+        h_last = placed("h_last", [P, CHUNK, PACK], BF16, 12288)
         h_codes = tile("h_codes", [P, J], U32)
         h_plane = tile("h_plane", [P, J], U8)
         w_dealt = tile("w_dealt", [P, PACK, P, 2], U8)
         w_plane_dealt = tile("w_plane_dealt", [P, PACK, P], U8)
         top = {k: tile("top%d" % k, [P, CHUNK, PACK], BF16) for k in (2, 3)}
+
+        def h_words(k, count=1):
+            return h_last[:] if k == LAST else h_bf[:, points(k, count), :]
 
         def points(k, count=1):
             return slice(CHUNK * k, CHUNK * (k + count))
@@ -123,9 +129,9 @@ def tile_list_pnet_bias_kernel(
             nc.gpsimd.tensor_copy(w_dealt[:], w_codes[:].bitcast(U8).rearrange("p (m t e) -> p t m e", t=PACK, e=2))
             nc.gpsimd.tensor_copy(w_plane_dealt[:], w_plane[:].bitcast(U8).rearrange("p (m t) -> p t m", t=PACK))
 
-        def round_wc():
-            dst = wc_bf[:].rearrange("p (t m) i -> p m i t", t=PACK)
-            nc.scalar.copy(dst, wc_raw[:].rearrange("p i (m t) -> p m i t", t=PACK))
+        def round_wc(u):
+            dst = wc_bf[:].rearrange("p (t m) i -> p m i t", t=PACK)[:, (P // 2) * u : (P // 2) * (u + 1)]
+            nc.scalar.copy(dst, wc_raw[u][:].rearrange("p i (m t) -> p m i t", t=PACK))
 
         def round_on_scalar(dst, src):
             nc.scalar.copy(
@@ -138,9 +144,9 @@ def tile_list_pnet_bias_kernel(
         def quantize(codes, plane, src):
             nc.vector.quantize_mx(out=codes.bitcast(FP8X4), scales=plane, in_=src.rearrange("p x i -> p (x i)"))
 
-        def quantize_columns(codes, plane, src, k, count=1):
+        def quantize_h(k, count=1):
             cols = points(k, count)
-            quantize(codes[:, cols], plane[:, cols], src[:, cols, :])
+            quantize(h_codes[:, cols], h_plane[:, cols], h_words(k, count))
 
         def by_points(bank):
             return bank[:].rearrange("j (t m) -> j t m", t=PACK)
@@ -219,7 +225,7 @@ def tile_list_pnet_bias_kernel(
             nc.scalar.activation(top[k][:], product_by_rows(bank, k, LAST, True), ACT.Relu)
 
         def larger_candidate(k):
-            flat = h_bf[:, points(k), :].rearrange("p j t -> p (j t)")
+            flat = h_words(k).rearrange("p j t -> p (j t)")
             nc.vector.tensor_tensor(flat, flat, top[k][:].rearrange("p j t -> p (j t)"), ALU.max)
 
         def product(step, bank):
@@ -237,7 +243,7 @@ def tile_list_pnet_bias_kernel(
             elif g is not None:
                 nc.vector.tensor_tensor(pooled_woven(k), sums, pooled_woven(k), ALU.max)
             else:
-                nc.vector.tensor_tensor(h_bf[:, points(k), :], sums, pooled_woven(k), ALU.add)
+                nc.vector.tensor_tensor(h_words(k), sums, pooled_woven(k), ALU.add)
 
         steps = [(0, 1), (1, 1), (0, 2), (1, 2), (0, 3), (2, 1), (1, 3), (3, 1), (2, 2), (3, 2), (2, None), (3, None)]
         waiting = []
@@ -265,7 +271,6 @@ def tile_list_pnet_bias_kernel(
             nc.vector.tensor_tensor(dst[:], sums, bias[:, lo:hi].unsqueeze(2).to_broadcast(list(sums.shape)), ALU.add)
 
         def second_layer(k, count, shares):
-            quantize_columns(h_codes, h_plane, h_bf, k, count)
             width = CHUNK * count
             cols = points(k, count)
             for bank, add_bias, queue, lo, hi in shares:
@@ -280,7 +285,10 @@ def tile_list_pnet_bias_kernel(
                         stop=True,
                     )
             for bank, add_bias, queue, lo, hi in shares:
-                result = tile("result%d_%d" % (k, lo), [P, hi - lo, width], F32)
+                if k == 2 and add_bias is bias_on_vector:
+                    result = placed("result_late", [P, hi - lo, width], F32, 12288)
+                else:
+                    result = tile("result%d_%d" % (k, lo), [P, hi - lo, width], F32)
                 sums = bank[:, 0 : width * (hi - lo)].rearrange("p (q j) -> p q j", j=width)
                 add_bias(result, sums, lo, hi)
                 queue.dma_start(out_rows[:, lo:hi, cols], result[:])
@@ -288,14 +296,14 @@ def tile_list_pnet_bias_kernel(
         gather_words(0, 2)
         gather_words(2, 2)
         deal_w()
-        round_wc()
+        round_wc(0)
+        round_wc(1)
         quantize(wc_codes[:], wc_plane[:], wc_bf[:])
         for k in range(2):
             nc.scalar.copy(first[k], neighbour_by_points(early_banks[k], k, 0))
-        round_on_gpsimd(c_bf[1][:], c_raw[:, :, HALF:J])
-        round_on_scalar(c_bf[0][:], c_raw[:, :, 0:HALF])
-        for u in (1, 0):
-            quantize(c_codes[:, HALF * u : HALF * (u + 1)], c_plane[:, HALF * u : HALF * (u + 1)], c_bf[u][:])
+        round_on_gpsimd(c_bf[:, C_ON_SCALAR:J, :], c_raw[:, :, C_ON_SCALAR:J])
+        round_on_scalar(c_bf[:, 0:C_ON_SCALAR, :], c_raw[:, :, 0:C_ON_SCALAR])
+        quantize(c_codes[:], c_plane[:], c_bf[:])
         round_on_gpsimd(wd_bf[:], wd_raw[:])
         for bank in fold_banks:
             start_product(bank)
@@ -318,10 +326,30 @@ def tile_list_pnet_bias_kernel(
         top_candidate(late_banks[1], 3)
         quantize(wd_codes[:], wd_plane[:], wd_bf[:])
         free_second = fold_next()
+        quantize_h(0, 2)
         second_layer(0, 2, [(free_first, bias_on_scalar, nc.sync, 0, 2), (early_banks[1], bias_on_scalar, nc.sync, 2, 4)])
         fold_next()
         fold_next()
         larger_candidate(2)
-        second_layer(2, 1, [(late_banks[0], bias_on_scalar, nc.sync, 0, 2), (late_banks[1], bias_on_scalar, nc.sync, 2, 4)])
         larger_candidate(3)
-        second_layer(3, 1, [(early_banks[0], bias_on_vector, nc.sync, 2, 4), (free_second, bias_on_scalar, nc.scalar, 0, 2)])
+        quantize_h(2)
+        quantize_h(3)
+        second_layer(2, 1, [(late_banks[0], bias_on_scalar, nc.sync, 0, 2), (late_banks[1], bias_on_vector, nc.sync, 2, 4)])
+        last_banks = [free_second, fold_banks[3], early_banks[0], early_banks[0]]
+        for q in (0, 2, 3, 1):
+            nc.tensor.matmul_mx(
+                out=last_banks[q][:, points(q)],
+                lhsT=wd_codes[:, P * q : P * (q + 1)].bitcast(FP8X4),
+                lhsT_scale=wd_plane[:, P * q : P * (q + 1)],
+                rhs=h_codes[:, points(LAST)].bitcast(FP8X4),
+                rhs_scale=h_plane[:, points(LAST)],
+                start=True,
+                stop=True,
+            )
+        low = tile("last_low", [P, 2, CHUNK], F32)
+        high = tile("last_high", [P, 2, CHUNK], F32)
+        bias_on_vector(high, early_banks[0][:, points(2, 2)].rearrange("p (q j) -> p q j", j=CHUNK), 2, 4)
+        nc.sync.dma_start(out_rows[:, 2:4, points(LAST)], high[:])
+        for q in range(2):
+            nc.scalar.activation(low[:, q, :], last_banks[q][:, points(q)], ACT.Identity, bias=bias[:, q : q + 1])
+        nc.scalar.dma_start(out_rows[:, 0:2, points(LAST)], low[:])

@@ -27,7 +27,7 @@ LINE = 4
 CHUNK = 128
 HALF = 256
 ROW_TILES = N // P
-C_ON_SCALAR = 320
+C_ON_SCALAR = 288
 LAST = G - 1
 
 
@@ -237,9 +237,7 @@ def tile_list_pnet_bias_kernel(
         def fold(step, sums):
             k, g = step
             if k < 2:
-                moves_at = LAST - k
-                so_far = first[k] if g <= moves_at else pooled[k]
-                nc.vector.tensor_tensor(first[k] if g < moves_at else pooled[k], sums, so_far, ALU.max)
+                nc.vector.tensor_tensor(first[k] if g < LAST else pooled[k], sums, first[k], ALU.max)
             elif g is not None:
                 nc.vector.tensor_tensor(pooled_woven(k), sums, pooled_woven(k), ALU.max)
             else:
@@ -324,8 +322,8 @@ def tile_list_pnet_bias_kernel(
         fold_next()
         free_first = fold_next()
         top_candidate(late_banks[1], 3)
-        quantize(wd_codes[:], wd_plane[:], wd_bf[:])
         free_second = fold_next()
+        quantize(wd_codes[:], wd_plane[:], wd_bf[:])
         quantize_h(0, 2)
         second_layer(0, 2, [(free_first, bias_on_scalar, nc.sync, 0, 2), (early_banks[1], bias_on_scalar, nc.sync, 2, 4)])
         fold_next()

@@ -109,7 +109,8 @@ def tile_list_pnet_bias_kernel(
         h_plane = tile("h_plane", [P, J], U8)
         w_dealt = tile("w_dealt", [P, PACK, P, 2], U8)
         w_plane_dealt = tile("w_plane_dealt", [P, PACK, P], U8)
-        top = {k: tile("top%d" % k, [P, CHUNK, PACK], BF16) for k in (2, 3)}
+        top = tile("top", [P, 2, HALF, 2], BF16)
+        summed = tile("summed", [P, 2, HALF, 2], BF16)
 
         def h_words(k, count=1):
             return h_last[:] if k == LAST else h_bf[:, points(k, count), :]
@@ -117,8 +118,8 @@ def tile_list_pnet_bias_kernel(
         def points(k, count=1):
             return slice(CHUNK * k, CHUNK * (k + count))
 
-        def entries(g, k):
-            return slice(J * g + CHUNK * k, J * g + CHUNK * (k + 1))
+        def entries(g, k, count=1):
+            return slice(J * g + CHUNK * k, J * g + CHUNK * (k + count))
 
         def gather_words(g, count):
             list_cols = slice(g * J // PER_COLUMN, (g + count) * J // PER_COLUMN)
@@ -194,15 +195,16 @@ def tile_list_pnet_bias_kernel(
             nc.scalar.activation(h_bf[:, points(k), :], woven_view(bank), ACT.Relu)
 
         def product_by_rows(bank, k, g, with_own):
-            for t in range(PACK):
-                dst = bank[:, CHUNK * t : CHUNK * (t + 1)]
+            for e in range(2):
+                t = 2 * (k - 2) + e
+                dst = bank[:, HALF * e : HALF * (e + 1)]
                 if g is not None:
                     nc.tensor.matmul_mx(
                         out=dst,
                         lhsT=w_dealt[:, t, :, :].rearrange("p m e -> p (m e)").bitcast(FP4X4),
                         lhsT_scale=w_plane_dealt[:, t, :],
-                        rhs=got_codes[:, entries(g, k)].bitcast(FP8X4),
-                        rhs_scale=got_plane[:, entries(g, k)],
+                        rhs=got_codes[:, entries(g, 2, 2)].bitcast(FP8X4),
+                        rhs_scale=got_plane[:, entries(g, 2, 2)],
                         start=True,
                         stop=not with_own,
                     )
@@ -211,22 +213,26 @@ def tile_list_pnet_bias_kernel(
                         out=dst,
                         lhsT=wc_codes[:, P * t : P * (t + 1)].bitcast(FP8X4),
                         lhsT_scale=wc_plane[:, P * t : P * (t + 1)],
-                        rhs=c_codes[:, points(k)].bitcast(FP8X4),
-                        rhs_scale=c_plane[:, points(k)],
+                        rhs=c_codes[:, points(2, 2)].bitcast(FP8X4),
+                        rhs_scale=c_plane[:, points(2, 2)],
                         start=g is None,
                         stop=True,
                     )
-            return woven_view(bank)
+            return bank[:].rearrange("p (e j) -> p j e", e=2)
 
         def pooled_woven(k):
-            return pooled[k].rearrange("p a b -> p (a b)").rearrange("p (j t) -> p j t", t=PACK)
+            return pooled[k].rearrange("p a b -> p (a b)").rearrange("p (j e) -> p j e", e=2)
 
         def top_candidate(bank, k):
-            nc.scalar.activation(top[k][:], product_by_rows(bank, k, LAST, True), ACT.Relu)
+            nc.scalar.activation(top[:, k - 2], product_by_rows(bank, k, LAST, True), ACT.Relu)
 
         def larger_candidate(k):
-            flat = h_words(k).rearrange("p j t -> p (j t)")
-            nc.vector.tensor_tensor(flat, flat, top[k][:].rearrange("p j t -> p (j t)"), ALU.max)
+            nc.vector.tensor_tensor(
+                h_words(k).rearrange("p j (u e) -> p j u e", e=2),
+                summed[:].rearrange("p u j e -> p j u e")[:, points(k - 2)],
+                top[:].rearrange("p u j e -> p j u e")[:, points(k - 2)],
+                ALU.max,
+            )
 
         def product(step, bank):
             k, g = step
@@ -240,8 +246,11 @@ def tile_list_pnet_bias_kernel(
                 nc.vector.tensor_tensor(first[k] if g < LAST else pooled[k], sums, first[k], ALU.max)
             elif g is not None:
                 nc.vector.tensor_tensor(pooled_woven(k), sums, pooled_woven(k), ALU.max)
+            elif k == 2:
+                nc.vector.tensor_tensor(summed[:, 0], sums, pooled_woven(k), ALU.add)
             else:
-                nc.vector.tensor_tensor(h_words(k), sums, pooled_woven(k), ALU.add)
+                for v in range(2):
+                    nc.vector.tensor_tensor(summed[:, 1, points(v)], sums[:, points(v)], pooled_woven(k)[:, points(v)], ALU.add)
 
         steps = [(0, 1), (1, 1), (0, 2), (1, 2), (0, 3), (2, 1), (1, 3), (3, 1), (2, 2), (3, 2), (2, None), (3, None)]
         waiting = []

@@ -27,7 +27,7 @@ LINE = 4
 CHUNK = 128
 HALF = 256
 ROW_TILES = N // P
-C_ON_SCALAR = 288
+C_ON_SCALAR = 256
 LAST = G - 1
 
 
@@ -243,7 +243,8 @@ def tile_list_pnet_bias_kernel(
         def fold(step, sums):
             k, g = step
             if k < 2:
-                nc.vector.tensor_tensor(first[k] if g < LAST else pooled[k], sums, first[k], ALU.max)
+                chain = [[first[0], first[0], first[0], pooled[0]], [first[1], first[1], pooled[1], pooled[1]]][k]
+                nc.vector.tensor_tensor(chain[g], sums, chain[g - 1], ALU.max)
             elif g is not None:
                 nc.vector.tensor_tensor(pooled_woven(k), sums, pooled_woven(k), ALU.max)
             elif k == 2:
@@ -252,7 +253,7 @@ def tile_list_pnet_bias_kernel(
                 for v in range(2):
                     nc.vector.tensor_tensor(summed[:, 1, points(v)], sums[:, points(v)], pooled_woven(k)[:, points(v)], ALU.add)
 
-        steps = [(0, 1), (1, 1), (0, 2), (1, 2), (0, 3), (2, 1), (1, 3), (3, 1), (2, 2), (3, 2), (2, None), (3, None)]
+        steps = [(0, 1), (1, 1), (0, 2), (1, 2), (0, 3), (1, 3), (2, 1), (3, 1), (2, 2), (3, 2), (2, None), (3, None)]
         waiting = []
 
         def start_product(bank):
@@ -325,8 +326,8 @@ def tile_list_pnet_bias_kernel(
         for _ in range(4):
             fold_next()
         fold_next(finish_in=early_banks[1])
-        fold_next()
         fold_next(finish_in=late_banks[0])
+        fold_next()
         top_candidate(early_banks[0], 2)
         fold_next()
         free_first = fold_next()

@@ -27,7 +27,7 @@ LINE = 4
 CHUNK = 128
 HALF = 256
 ROW_TILES = N // P
-C_ON_SCALAR = 256
+C_ON_SCALAR = 320
 LAST = G - 1
 
 

@@ -27,7 +27,7 @@ LINE = 4
 CHUNK = 128
 HALF = 256
 ROW_TILES = N // P
-C_ON_SCALAR = 320
+C_ON_SCALAR = 288
 LAST = G - 1
 
 

@@ -311,7 +311,8 @@ def tile_list_pnet_bias_kernel(
             nc.scalar.copy(first[k], neighbour_by_points(early_banks[k], k, 0))
         round_on_gpsimd(c_bf[:, C_ON_SCALAR:J, :], c_raw[:, :, C_ON_SCALAR:J])
         round_on_scalar(c_bf[:, 0:C_ON_SCALAR, :], c_raw[:, :, 0:C_ON_SCALAR])
-        quantize(c_codes[:], c_plane[:], c_bf[:])
+        for u in range(2):
+            quantize(c_codes[:, points(2 * u, 2)], c_plane[:, points(2 * u, 2)], c_bf[:, points(2 * u, 2), :])
         round_on_gpsimd(wd_bf[:], wd_raw[:])
         for bank in fold_banks:
             start_product(bank)

from contextlib import ExitStack

import concourse.mybir as mybir
from concourse.masks import make_identity

K, R, N, T, J, G = 512, 512, 512, 4096, 512, 4
FLOPS = 2 * K * R * J * (G + 1) + 2 * R * N * J

F32 = mybir.dt.float32
BF16 = mybir.dt.bfloat16
I32 = mybir.dt.int32
U32 = mybir.dt.uint32
U16 = mybir.dt.uint16
U8 = mybir.dt.uint8
FP8X4 = mybir.dt.float8_e4m3fn_x4
FP4X4 = mybir.dt.float4_e2m1fn_x4
ALU = mybir.AluOpType
ACT = mybir.ActivationFunctionType

P = 128
PACK = 4
QUADRANT = 32
PLANE_ROWS = 4
SCALE_ROWS = K // 32
PER_COLUMN = 16
LINE = 4
CHUNK = 128
HALF = 256
ROW_TILES = N // P
C_ON_SCALAR = 288
LAST = G - 1


def tile_list_pnet_bias_kernel(
    tc, tab_words, tab_scales, c, w_words, w_scales, wc, wd, b, offs, out
):
    nc = tc.nc
    with ExitStack() as ctx:
        sb = ctx.enter_context(tc.tile_pool(name="sb", bufs=1))
        shared = ctx.enter_context(tc.tile_pool(name="shared", bufs=1))
        ps = ctx.enter_context(tc.psum_pool(name="ps", bufs=1))

        def tile(name, shape, dtype):
            return sb.tile(shape, dtype, name=name, align_bytes=64)

        offsets = sb.tile([P, G * J // PER_COLUMN], U16, name="offsets")
        tab_rows = tile("tab_rows", [P, T // 4], I32)
        tab_codes = tile("tab_codes", [P, T], I32)
        w_plane = tile("w_plane", [P, R // 4], I32)
        w_codes = tile("w_codes", [P, R // 2], I32)
        bias = tile("bias", [P, ROW_TILES], F32)
        ident = tile("ident", [P, P], F32)
        got_rows = tile("got_rows", [P, G * J], U8)
        got_plane = tile("got_plane", [P, G * J], U8)
        got_codes = tile("got_codes", [P, G * J], U32)

        def load_rows(name, src, lo, hi):
            raw = tile(name, [P, PACK, hi - lo], F32)
            nc.sync.dma_start(raw[:], src.rearrange("(p i) x -> p i x", i=PACK)[:, :, lo:hi])
            return raw

        def plane_rows(r):
            return slice(r, P, QUADRANT)

        nc.gpsimd.memset(w_plane[:], 0)
        make_identity(nc, ident[:])
        first_row = P - SCALE_ROWS
        nc.vector.memset(tab_rows[0:first_row, :], 0)
        nc.sync.dma_start(tab_rows[first_row:P, :], tab_scales[0].bitcast(I32))
        nc.sync.dma_start(offsets[:], offs)
        nc.sync.dma_start(tab_codes[:], tab_words[0].rearrange("p t i -> p (t i)").bitcast(I32))
        for r in range(PLANE_ROWS):
            nc.sync.dma_start(w_plane[plane_rows(r), :], w_scales[0, r:SCALE_ROWS:PLANE_ROWS, :].bitcast(I32))
        nc.sync.dma_start(w_codes[:], w_words[0].bitcast(I32))
        wc_raw = [load_rows("wc_raw%d" % u, wc, HALF * u, HALF * (u + 1)) for u in range(2)]
        nc.vector.tensor_copy(got_rows[:], tab_rows[:].bitcast(U8).indirect(offsets[:]))
        for r in range(PLANE_ROWS):
            rows = slice(first_row + r, P, PLANE_ROWS)
            nc.sync.dma_start(got_plane[plane_rows(r), :].bitcast(I32), got_rows[rows, :].bitcast(I32))
        c_raw = load_rows("c_raw", c, 0, J)
        wd_raw = load_rows("wd_raw", wd, 0, N)
        with nc.allow_non_contiguous_dma(reason="one bias value a partition and row tile"):
            nc.sync.dma_start(bias[:], b.rearrange("(q p) -> p q", p=P))

        banks = [ps.tile([P, R], F32, name="bank%d" % i) for i in range(8)]
        early_banks, fold_banks, late_banks = banks[0:2], banks[2:6], banks[6:8]

        def placed(name, shape, dtype, offset):
            return shared.tile(shape, dtype, name=name, align_bytes=64, offset=offset)

        wc_bf = placed("wc_bf", [P, R, PACK], BF16, 0)
        c_bf = placed("c_bf", [P, J, PACK], BF16, 2048)
        wd_bf = placed("wd_bf", [P, N, PACK], BF16, 0)
        second = placed("second", [P, 2, PACK, P], F32, 4096)
        spent = wc_raw[1][:].rearrange("p (k a) (b m) -> p k (a b) m", k=2, m=P)
        first = [spent[:, 0], spent[:, 1]]
        pooled = [second[:, 0], second[:, 1]]
        pooled.extend(c_raw[:, i, :].rearrange("p (e m) -> p e m", m=P) for i in range(2))
        own = [tile("own%d" % k, [P, PACK, P], F32) for k in range(2)]
        wc_codes = tile("wc_codes", [P, R], U32)
        wc_plane = tile("wc_plane", [P, R], U8)
        c_codes = tile("c_codes", [P, J], U32)
        c_plane = tile("c_plane", [P, J], U8)
        wd_codes = tile("wd_codes", [P, N], U32)
        wd_plane = tile("wd_plane", [P, N], U8)
        h_bf = tile("h_bf", [P, J - CHUNK, PACK], BF16)
        h_last = placed("h_last", [P, CHUNK, PACK], BF16, 12288)
        h_codes = tile("h_codes", [P, J], U32)
        h_plane = tile("h_plane", [P, J], U8)
        w_dealt = tile("w_dealt", [P, PACK, P, 2], U8)
        w_plane_dealt = tile("w_plane_dealt", [P, PACK, P], U8)
        top = tile("top", [P, 2, HALF, 2], BF16)
        summed = tile("summed", [P, 2, HALF, 2], BF16)

        def h_words(k, count=1):
            return h_last[:] if k == LAST else h_bf[:, points(k, count), :]

        def points(k, count=1):
            return slice(CHUNK * k, CHUNK * (k + count))

        def entries(g, k, count=1):
            return slice(J * g + CHUNK * k, J * g + CHUNK * (k + count))

        def gather_words(g, count):
            list_cols = slice(g * J // PER_COLUMN, (g + count) * J // PER_COLUMN)
            picked = tab_codes[:].bitcast(U32).indirect(offsets[:, list_cols])
            nc.vector.tensor_copy(got_codes[:, g * J : (g + count) * J], picked)

        def deal_w():
            nc.gpsimd.tensor_copy(w_dealt[:], w_codes[:].bitcast(U8).rearrange("p (m t e) -> p t m e", t=PACK, e=2))
            nc.gpsimd.tensor_copy(w_plane_dealt[:], w_plane[:].bitcast(U8).rearrange("p (m t) -> p t m", t=PACK))

        def round_wc(u):
            dst = wc_bf[:].rearrange("p (t m) i -> p m i t", t=PACK)[:, (P // 2) * u : (P // 2) * (u + 1)]
            nc.scalar.copy(dst, wc_raw[u][:].rearrange("p i (m t) -> p m i t", t=PACK))

        def round_on_scalar(dst, src):
            nc.scalar.copy(
                dst.rearrange("p (x u) i -> p x i u", u=LINE), src.rearrange("p i (x u) -> p x i u", u=LINE)
            )

        def round_on_gpsimd(dst, src):
            nc.gpsimd.tensor_scalar(dst, src.rearrange("p i x -> p x i"), 1.0, 0.0, ALU.mult, ALU.add)

        def quantize(codes, plane, src):
            nc.vector.quantize_mx(out=codes.bitcast(FP8X4), scales=plane, in_=src.rearrange("p x i -> p (x i)"))

        def quantize_h(k, count=1):
            cols = points(k, count)
            quantize(h_codes[:, cols], h_plane[:, cols], h_words(k, count))

        def by_points(bank):
            return bank[:].rearrange("j (t m) -> j t m", t=PACK)

        def neighbour_by_points(bank, k, g):
            nc.tensor.matmul_mx(
                out=bank[:],
                lhsT=got_codes[:, entries(g, k)].bitcast(FP8X4),
                lhsT_scale=got_plane[:, entries(g, k)],
                rhs=w_dealt[:].rearrange("p t m e -> p (t m e)").bitcast(FP4X4),
                rhs_scale=w_plane_dealt[:].rearrange("p t m -> p (t m)"),
                start=True,
                stop=True,
            )
            return by_points(bank)

        def own_by_points(bank, k):
            nc.tensor.matmul_mx(
                out=bank[:],
                lhsT=c_codes[:, points(k)].bitcast(FP8X4),
                lhsT_scale=c_plane[:, points(k)],
                rhs=wc_codes[:].bitcast(FP8X4),
                rhs_scale=wc_plane[:],
                start=True,
                stop=True,
            )
            nc.scalar.copy(own[k][:], by_points(bank))

        def woven_view(bank):
            return bank[:].rearrange("p (t j) -> p j t", t=PACK)

        def transpose_into(bank, src, opens):
            for t in range(PACK):
                nc.tensor.matmul(
                    bank[:, CHUNK * t : CHUNK * (t + 1)],
                    src[:, t, :],
                    ident[:],
                    is_transpose=True,
                    start=(opens and t == 0),
                    stop=(not opens and t == PACK - 1),
                )

        def finish_by_points(bank, k):
            transpose_into(bank, pooled[k], False)
            nc.scalar.activation(h_bf[:, points(k), :], woven_view(bank), ACT.Relu)

        def product_by_rows(bank, k, g, with_own):
            for e in range(2):
                t = 2 * (k - 2) + e
                dst = bank[:, HALF * e : HALF * (e + 1)]
                if g is not None:
                    nc.tensor.matmul_mx(
                        out=dst,
                        lhsT=w_dealt[:, t, :, :].rearrange("p m e -> p (m e)").bitcast(FP4X4),
                        lhsT_scale=w_plane_dealt[:, t, :],
                        rhs=got_codes[:, entries(g, 2, 2)].bitcast(FP8X4),
                        rhs_scale=got_plane[:, entries(g, 2, 2)],
                        start=True,
                        stop=not with_own,
                    )
                if with_own:
                    nc.tensor.matmul_mx(
                        out=dst,
                        lhsT=wc_codes[:, P * t : P * (t + 1)].bitcast(FP8X4),
                        lhsT_scale=wc_plane[:, P * t : P * (t + 1)],
                        rhs=c_codes[:, points(2, 2)].bitcast(FP8X4),
                        rhs_scale=c_plane[:, points(2, 2)],
                        start=g is None,
                        stop=True,
                    )
            return bank[:].rearrange("p (e j) -> p j e", e=2)

        def pooled_woven(k):
            return pooled[k].rearrange("p a b -> p (a b)").rearrange("p (j e) -> p j e", e=2)

        def top_candidate(bank, k):
            nc.scalar.activation(top[:, k - 2], product_by_rows(bank, k, LAST, True), ACT.Relu)

        def larger_candidate(k):
            nc.vector.tensor_tensor(
                h_words(k).rearrange("p j (u e) -> p j u e", e=2),
                summed[:].rearrange("p u j e -> p j u e")[:, points(k - 2)],
                top[:].rearrange("p u j e -> p j u e")[:, points(k - 2)],
                ALU.max,
            )

        def product(step, bank):
            k, g = step
            if k < 2:
                return neighbour_by_points(bank, k, g)
            return product_by_rows(bank, k, g, g is None)

        def fold(step, sums):
            k, g = step
            if k < 2:
                chain = [[first[0], first[0], first[0], pooled[0]], [first[1], first[1], pooled[1], pooled[1]]][k]
                nc.vector.tensor_tensor(chain[g], sums, chain[g - 1], ALU.max)
            elif g is not None:
                nc.vector.tensor_tensor(pooled_woven(k), sums, pooled_woven(k), ALU.max)
            elif k == 2:
                nc.vector.tensor_tensor(summed[:, 0], sums, pooled_woven(k), ALU.add)
            else:
                for v in range(2):
                    nc.vector.tensor_tensor(summed[:, 1, points(v)], sums[:, points(v)], pooled_woven(k)[:, points(v)], ALU.add)

        steps = [(0, 1), (1, 1), (0, 2), (1, 2), (0, 3), (1, 3), (2, 1), (3, 1), (2, 2), (3, 2), (2, None), (3, None)]
        waiting = []

        def start_product(bank):
            step = steps.pop(0)
            waiting.append((step, bank, product(step, bank)))

        def fold_next(finish_in=None):
            step, bank, sums = waiting.pop(0)
            fold(step, sums)
            if finish_in is not None:
                finish_by_points(finish_in, step[0])
            if steps:
                start_product(bank)
            return bank

        out_rows = out.rearrange("(q p) j -> p q j", p=P)

        def bias_on_scalar(dst, sums, lo, hi):
            for q in range(lo, hi):
                nc.scalar.activation(dst[:, q - lo, :], sums[:, q - lo, :], ACT.Identity, bias=bias[:, q : q + 1])

        def bias_on_vector(dst, sums, lo, hi):
            nc.vector.tensor_tensor(dst[:], sums, bias[:, lo:hi].unsqueeze(2).to_broadcast(list(sums.shape)), ALU.add)

        def second_layer(k, count, shares):
            width = CHUNK * count
            cols = points(k, count)
            for bank, add_bias, queue, lo, hi in shares:
                for q in range(lo, hi):
                    nc.tensor.matmul_mx(
                        out=bank[:, width * (q - lo) : width * (q - lo + 1)],
                        lhsT=wd_codes[:, P * q : P * (q + 1)].bitcast(FP8X4),
                        lhsT_scale=wd_plane[:, P * q : P * (q + 1)],
                        rhs=h_codes[:, cols].bitcast(FP8X4),
                        rhs_scale=h_plane[:, cols],
                        start=True,
                        stop=True,
                    )
            for bank, add_bias, queue, lo, hi in shares:
                if k == 2 and add_bias is bias_on_vector:
                    result = placed("result_late", [P, hi - lo, width], F32, 12288)
                else:
                    result = tile("result%d_%d" % (k, lo), [P, hi - lo, width], F32)
                sums = bank[:, 0 : width * (hi - lo)].rearrange("p (q j) -> p q j", j=width)
                add_bias(result, sums, lo, hi)
                queue.dma_start(out_rows[:, lo:hi, cols], result[:])

        gather_words(0, 2)
        gather_words(2, 2)
        deal_w()
        round_wc(0)
        round_wc(1)
        quantize(wc_codes[:], wc_plane[:], wc_bf[:])
        for k in range(2):
            nc.scalar.copy(first[k], neighbour_by_points(early_banks[k], k, 0))
        round_on_gpsimd(c_bf[:, C_ON_SCALAR:J, :], c_raw[:, :, C_ON_SCALAR:J])
        round_on_scalar(c_bf[:, 0:C_ON_SCALAR, :], c_raw[:, :, 0:C_ON_SCALAR])
        for u in range(2):
            quantize(c_codes[:, points(2 * u, 2)], c_plane[:, points(2 * u, 2)], c_bf[:, points(2 * u, 2), :])
        round_on_gpsimd(wd_bf[:], wd_raw[:])
        for bank in fold_banks:
            start_product(bank)

        own_by_points(early_banks[0], 0)
        own_by_points(early_banks[1], 1)
        transpose_into(early_banks[1], own[0], True)
        nc.scalar.copy(pooled_woven(2), product_by_rows(late_banks[0], 2, 0, False))
        transpose_into(late_banks[0], own[1], True)
        nc.scalar.copy(pooled_woven(3), product_by_rows(late_banks[1], 3, 0, False))

        for _ in range(4):
            fold_next()
        fold_next(finish_in=early_banks[1])
        fold_next(finish_in=late_banks[0])
        fold_next()
        top_candidate(early_banks[0], 2)
        fold_next()
        free_first = fold_next()
        top_candidate(late_banks[1], 3)
        free_second = fold_next()
        quantize(wd_codes[:], wd_plane[:], wd_bf[:])
        quantize_h(0, 2)
        second_layer(0, 2, [(free_first, bias_on_scalar, nc.sync, 0, 2), (early_banks[1], bias_on_scalar, nc.sync, 2, 4)])
        fold_next()
        fold_next()
        larger_candidate(2)
        larger_candidate(3)
        quantize_h(2)
        quantize_h(3)
        second_layer(2, 1, [(late_banks[0], bias_on_scalar, nc.sync, 0, 2), (late_banks[1], bias_on_vector, nc.sync, 2, 4)])
        last_banks = [free_second, fold_banks[3], early_banks[0], early_banks[0]]
        for q in (0, 2, 3, 1):
            nc.tensor.matmul_mx(
                out=last_banks[q][:, points(q)],
                lhsT=wd_codes[:, P * q : P * (q + 1)].bitcast(FP8X4),
                lhsT_scale=wd_plane[:, P * q : P * (q + 1)],
                rhs=h_codes[:, points(LAST)].bitcast(FP8X4),
                rhs_scale=h_plane[:, points(LAST)],
                start=True,
                stop=True,
            )
        low = tile("last_low", [P, 2, CHUNK], F32)
        high = tile("last_high", [P, 2, CHUNK], F32)
        bias_on_vector(high, early_banks[0][:, points(2, 2)].rearrange("p (q j) -> p q j", j=CHUNK), 2, 4)
        nc.sync.dma_start(out_rows[:, 2:4, points(LAST)], high[:])
        for q in range(2):
            nc.scalar.activation(low[:, q, :], last_banks[q][:, points(q)], ACT.Identity, bias=bias[:, q : q + 1])
        nc.scalar.dma_start(out_rows[:, 0:2, points(LAST)], low[:])
